import numpy as np, ml_dtypes
CORES = [9,25,41,57]
N = 4
BF = ml_dtypes.bfloat16
V, M, L, P, TV, HS = 4096, 2048, 256, 16, 6, (1, 2, 4, 8)
def pushed(ls, s, n):
    return np.take_along_axis(ls.reshape(N, 8, 16 * M), (s & 15) * M + (((s * s >> 5) + s + 77 * n) & (M - 1)), 2)
def parts(rng):
    kd = rng.permutation(np.arange(V) & 3); pool = np.argsort(kd, kind="stable").reshape(4, V >> 2)
    own = np.where(rng.random((N, 8, V)) < 0.02, rng.integers(0, 4, (N, 8, V)), kd); proto = rng.integers(0, 16, (N, 8, 16, 4))
    x = np.clip(np.take_along_axis(proto, own[:, :, None], 3) + rng.integers(-1, 2, (N, 8, 16, V)), 0, 15)
    ls = rng.integers(0, V, (N, 8, 16, M)); s = rng.integers(0, 4096, (N, 8, L))
    n = np.where(rng.random((N, 8, L)) < 0.5, rng.integers(15, 17, (N, 8, L)), rng.integers(0, 17, (N, 8, L)))
    return kd, pool, x, ls, s, n, rng.integers(10, 30, (N, 8)), rng.integers(0, 256, (N, 8, 16))
def spell(rng, ls, s, n, kd, pool, p):
    a = kd[pushed(ls, s, n)]; b = (a + rng.integers(1, 4, a.shape)) & 3; j = np.arange(1, 17)[:, None]; sh = (N, 8, 16, L)
    k = np.where(j % np.maximum(p, 1)[:, :, None] == 0, a[:, :, None], b[:, :, None])
    cut = np.maximum(2 * p, rng.integers(0, 17, p.shape))[:, :, None]
    k = np.where((p[:, :, None] == 0) | (j >= cut), rng.integers(0, 4, sh), k)
    return pool[k, rng.integers(0, V >> 2, sh)]
def two(a, b, p):
    j = np.arange(1, 17)[:, None]; q = np.where(p == 0, 99, p)[:, :, None]
    return np.where(j % q == 0, a[:, :, None], b[:, :, None])
def pack(x, ls, w, s, n, th, wt):
    w = np.where(np.arange(16)[:, None] < n[:, :, None, :], w, 0)
    return {"x": np.ascontiguousarray(x.reshape(N, 128, V)).astype(np.float32).astype(BF), "ls": np.ascontiguousarray(ls.reshape(N, 128, M)).astype(np.int32),
            "wd": np.ascontiguousarray(w.reshape(N, 128, L)).astype(np.int32), "nl": n.astype(np.int32), "sd": s.astype(np.int32),
            "th": np.ascontiguousarray(th.reshape(N, 8, 1)).astype(np.int32), "wt": np.ascontiguousarray(wt.reshape(N, 128, 1)).astype(np.int32)}
def setup_inputs(rng):
    kd, pool, x, ls, s, n, th, wt = parts(rng); p = rng.choice(np.array((0, 0) + HS), (N, 8, L))
    return pack(x, ls, spell(rng, ls, s, n, kd, pool, p), s, n, th, wt)
def setup_inputs_corners(rng):
    kd, pool, x, ls, s, n, th, wt = parts(rng); sh = (N, 8, L)
    ls = np.where(rng.random(ls.shape) < 0.2, rng.choice(np.array([0, V - 1]), ls.shape), ls)
    edge = np.array(sorted({0, 1, 15, 16} | {2 * h - 2 for h in HS} | {2 * h - 1 for h in HS})); p = rng.choice(np.array(HS), sh); u = rng.random(sh)
    n = np.where(u < 0.4, 2 * p - 2, np.where(u < 0.7, 2 * p - 1, rng.choice(edge, sh)))
    n[0, 0] = 0; n[N - 1, 7] = 16; n[:, 3] = rng.choice(np.array([0, 16]), (N, L))
    s = np.where(rng.random(sh) < 0.3, rng.choice(np.array([0, 15, 16, 4095]), sh), s)
    th = rng.choice(np.array([0, 1, 20, 240]), (N, 8)); wt = rng.choice(np.array([0, 1, 255]), (N, 8, 16))
    p[N - 1, 7] = 8; th[N - 1, 7] = 0
    c = int(rng.integers(1, N - 1))
    x[c] = 8 * (np.arange(V) & 1) + rng.integers(0, 3, (8, 16, V)); th[c] = 8; th[c - 1] = 240
    ls[c - 1] |= 1; ls[c] -= ls[c] & 1
    n[c - 1] = 0; n[c] = np.maximum(n[c], 1); n[c, 7, L - 1] = 0
    a = pushed(ls, s, n); u = rng.integers(0, 4, sh); own = P * np.arange(L) + rng.integers(0, P, sh)
    b = np.where(u == 0, 0, np.where(u == 1, V - 1, np.where(u == 2, own, rng.integers(0, V, sh))))
    w = two(a, b, p); w[c, :, 0] = a[c]
    return pack(x, ls, w, s, n, th, wt)
def setup_inputs_ties(rng):
    kd, pool, x, ls, s, n, th, wt = parts(rng); sh = (N, 8, L); half = V >> 3
    th = rng.integers(16, 61, (N, 8)); val = np.stack([0 * th, th, th + 1, 2 * th + 1], -1)
    loose = np.ones(V, np.int64); loose[pool[:, :half]] = 0
    e = val[:, :, kd] + loose * rng.integers(0, 17, (N, 8, V)); x = (e[:, :, None] + np.arange(16)[:, None]) >> 4
    ls = np.where(rng.random(ls.shape) < 0.8, pool[rng.integers(0, 4, ls.shape), rng.integers(0, half, ls.shape)], ls)
    p = rng.choice(np.array(HS), sh); a = kd[pushed(ls, s, n)]; b = np.array([3, 3, 0, 0])[a]
    c = np.where(rng.random(sh) < 0.6, np.array([1, 0, 3, 2])[a], np.array([2, 3, 0, 1])[a])
    k = np.where(np.arange(1, 17)[:, None] == p[:, :, None], c[:, :, None], two(a, b, p))
    return pack(x, ls, pool[k, rng.integers(0, half, k.shape)], s, n, th, wt)
def setup_inputs_again(rng):
    kd, pool, x, ls, s, n, th, wt = parts(rng)
    few = np.concatenate([np.arange(4 * P), V - 4 * P + np.arange(4 * P)])
    x = np.clip(rng.integers(0, 16, (N, 8, 16, 1)) + rng.integers(-3, 4, (N, 8, 16, V)), 0, 15); th = rng.integers(24, 44, (N, 8))
    ls = few[rng.integers(0, 8 * P, ls.shape)]; w = few[rng.integers(0, 8 * P, (N, 8, 16, L))]
    q = int(rng.integers(0, N)); n[q] = np.maximum(n[q], 1); w[q, :, 0] = pushed(ls, s, n)[q]
    return pack(x, ls, w, s, n, th, wt)
def setup_inputs_spread(rng):
    sh = (N, 8, L)
    x = np.minimum((np.exp2(4 * rng.random((N, 8, 1, V))) * rng.random((N, 8, 16, V))).astype(np.int64), 15)
    ls = np.minimum((V * rng.random((N, 8, 16, M)) * np.sqrt(rng.random((N, 8, 16, M)))).astype(np.int64), V - 1)
    w = np.minimum((np.exp2(np.log2(V) * rng.random((N, 8, 16, L)))).astype(np.int64), V - 1)
    s = np.where(rng.random(sh) < 0.5, rng.integers(0, 4096, sh), np.minimum(np.exp2(12 * rng.random(sh)).astype(np.int64), 4095))
    wt = np.minimum(np.exp2(8 * rng.random((N, 8, 16))).astype(np.int64) - 1, 255)
    return pack(x, ls, w, s, rng.integers(0, 17, sh), rng.integers(0, 241, (N, 8)), wt)
def setup_inputs_ends(rng):
    sh = (N, 8, L)
    u = rng.integers(0, 3, (N, 8, 1, V)); x = 15 * np.where(u == 2, rng.integers(0, 2, (N, 8, 16, V)), u)
    x[:, 1:7:2, :, 0] = 0; x[:, 1:7:2, :, V - 1] = 15; x[:, 7, :, 0] = 0; x[:, 7, :, V - 1] = 15; x[:, 0, :, 0] = 15; x[:, 0, :, V - 1] = 0
    ls = (V - 1) * rng.integers(0, 2, (N, 8, 16, M)); s = 4095 * rng.integers(0, 2, sh); n = 16 * (rng.random(sh) < 0.75).astype(np.int64)
    th = 240 * rng.integers(0, 2, (N, 8)); th[:, 7] = 0; th[:, 6] = 240
    wt = 255 * rng.integers(0, 2, (N, 8, 16)); wt[:, 7] = 255; wt[:, 0] = 0
    p = rng.choice(np.array((0,) + HS), sh)
    for i, k in ((0, 0), (1, 8), (7, 0), (10, 8), (L - 2, 8), (L - 1, 0)):
        s[:, 7, i] = 4095; n[:, 7, i] = 16; p[:, 7, i] = k
    ls[:, 7, 15, ((4095 * 4095 >> 5) + 4095 + 77 * 16) & (M - 1)] = V - 1
    a = pushed(ls, s, n)
    return pack(x, ls, two(a, V - 1 - a, p), s, n, th, wt)
def check_inputs(d):
    bad = []
    for k, lo, hi in (("x", 0, 15), ("ls", 0, V - 1), ("wd", 0, V - 1), ("nl", 0, 16), ("sd", 0, 4095), ("th", 0, 240), ("wt", 0, 255)):
        v = np.asarray(d[k]).astype(np.float64)
        if not np.all((v >= lo) & (v <= hi)): bad.append("range of " + k)
        if not np.all(v == np.floor(v)): bad.append("whole numbers in " + k)
    w = np.asarray(d["wd"]).reshape(N, 8, 16, L); n = np.asarray(d["nl"]).reshape(N, 8, 1, L)
    if np.any((np.arange(16)[:, None] >= n) & (w != 0)): bad.append("empty rows of wd")
    return bad
def reference(x, ls, wd, nl, sd, th, wt):
    X = x.astype(np.float32).astype(np.int32).reshape(N, 8, 16, V); tab = ls.astype(np.int64).reshape(N, 8, 16 * M)
    w = wd.astype(np.int64).reshape(N, 8, 16, L); n = nl.astype(np.int64); s = sd.astype(np.int64)
    lim = th.astype(np.int64).reshape(N, 8, 1, 1); wgt = wt.astype(np.int64).reshape(N, 8, 16, 1)
    A = np.zeros(N, np.int64); row = np.arange(16)[:, None]
    for t in range(TV):
        new = np.take_along_axis(tab, (s & 15) * M + (((s * s >> 5) + s + 77 * n) & (M - 1)), 2)
        w = np.concatenate([new[:, :, None], w[:, :, :15]], axis=2); n = np.minimum(n + 1, 16)
        G = np.take_along_axis(X, w.reshape(N, 8, 1, 16 * L), 3).reshape(N, 8, 16, 16, L)
        bound = lim + (A & 15).reshape(N, 1, 1, 1); h = np.zeros((N, 8, L), np.int64)
        for k in HS:
            D = np.add.reduce(np.abs(G[:, :, :, :k] - G[:, :, :, k:2 * k]), axis=2)
            h = np.where((h == 0) & (2 * k <= n) & np.all(D <= bound, axis=2), k, h)
        hit = h > 0
        z = np.maximum.reduce(np.where(row < h[:, :, None, None, :], G, 0), axis=3)
        tot = np.add.reduce(wgt * np.where(hit[:, :, None], z, G[:, :, :, 0]), axis=2)
        s = np.where(hit, tot + h, 5 * s + tot) & 4095
        at = row + h[:, :, None, :]
        w = np.where(at < 16, np.take_along_axis(w, np.minimum(at, 15), 2), 0); n = n - h
        col = np.roll(P * np.arange(L) + (s & (P - 1)), 1, axis=0)[:, :, None]
        old = np.take_along_axis(X, col, 3)
        val = np.where(np.roll(hit, 1, axis=0)[:, :, None], (old + np.roll(z, 1, axis=0)) >> 1, old)
        np.put_along_axis(X, col, val.astype(np.int32), 3)
        A = np.add.reduce(hit.astype(np.int64).reshape(N, 8 * L), axis=1)
        if t < TV - 1:
            by = 1 + (t + 1) // N - t // N
            w, n, s = [np.roll(np.roll(v, 1, axis=0), by, axis=1) for v in (w, n, s)]
    return {"yx": X.reshape(N, 128, V).astype(np.float32).astype(BF), "yw": w.reshape(N, 128, L).astype(np.float32), "yn": n.astype(np.float32), "ys": s.astype(np.float32)}

@@ -1,0 +1,589 @@
+from concourse.bass import DstId
+from concourse.mybir import AluOpType, AxisListType, ActivationFunctionType
+
+OP = AluOpType
+FN = ActivationFunctionType
+SIG = [0, 1, 2, 3, 5, 6]
+TV = 6
+POS = {(8, 0): 0, (8, 1): 1, (4, 0): 2, (8, 2): 3, (8, 3): 4, (4, 1): 5, (2, 0): 6,
+       (8, 4): 7, (8, 5): 8, (4, 2): 9, (8, 6): 10, (8, 7): 11, (4, 3): 12, (2, 1): 13, (1, 0): 14}
+SHORT = [(2, 1), (4, 1), (4, 3), (4, 2), (1, 0), (2, 0), (4, 0)]
+LONG = [1, 3, 5, 7, 2, 6, 0, 4]
+
+SCRATCH = {}
+TILE = {}
+_ARENA = {"int32": "ari", "float32": "arf", "bfloat16": "arb", "float16": "arh", "uint16": "aru"}
+_USED = {k: 0 for k in _ARENA}
+
+
+def _b(name, cols, dtype, where="sbuf"):
+    if where == "sbuf" and name[0] not in "XYZ" and name[:2] not in ("SX", "SY", "SZ") and name != "xt":
+        TILE[name] = (_ARENA[dtype], _USED[dtype], cols)
+        _USED[dtype] += (cols + 15) // 16 * 16
+        SCRATCH[_ARENA[dtype]] = ("sbuf", [128, _USED[dtype]], dtype)
+    else:
+        TILE[name] = (name, 0, cols)
+        SCRATCH[name] = (where, [128, cols], dtype)
+
+
+for _n, _c in (("lsi", 2048), ("wdi", 256), ("sdi", 256), ("nli", 256), ("thi", 8), ("wti", 8), ("ioi", 256), ("pi", 16), ("gi", 256),
+               ("g96", 96), ("lli", 96), ("llh", 96), ("vI", 16), ("hI", 16), ("hJ", 16), ("mI", 16), ("sI", 16), ("rI", 16), ("loI", 16), ("sq", 16), ("sq5", 16), ("w1", 16),
+               ("kI", 16), ("cc", 16), ("cI", 16), ("nv", 256), ("amI", 8), ("amJ", 8), ("xii", 256)):
+    _b(_n, _c, "int32")
+for _n, _c in (("lsf", 2048), ("sdf", 256), ("nlf", 256), ("pc", 32), ("xi", 256), ("fi", 128), ("If", 128), ("onf", 128),
+               ("thd", 96), ("thB", 96), ("base", 16), ("zbase", 16), ("d0s", 256), ("l15f", 16),
+               ("colf", 16), ("dg", 256), ("lsc", 256), ("np1", 16), ("en", 64), ("thr", 64), ("B1", 16), ("Bt", 240), ("amc", 8),
+               ("u0", 16), ("u1", 16), ("u2", 16), ("u3", 16), ("u4", 16), ("u5", 16), ("u6", 16),
+               ("zf", 16), ("M4", 16), ("cnt", 8), ("nB", 16), ("acc", 256), ("sfo", 16), ("ywx", 256), ("yws", 256), ("yns", 512)):
+    _b(_n, _c, "float32")
+for _n, _c in (("xt", 8192), ("I", 128), ("NI", 128), ("I5", 128), ("rh0", 256), ("rh1", 256), ("mask", 256), ("zr", 2048), ("mc", 80), ("lc", 128), ("on", 96), ("onm", 96),
+               ("wtb", 96), ("G8", 2048), ("Zp", 2064), ("d8", 2304), ("r8", 2048),
+               ("pen0", 256), ("pen1", 256), ("pen2", 256), ("pen4", 256), ("pen8", 256), ("N0", 128), ("N1", 128), ("N2", 128), ("ab", 1792), ("sm", 256), ("good", 240), ("m1", 112), ("m2", 48), ("b8", 16), ("rh", 256), ("rl", 256), ("rq", 256)):
+    _b(_n, _c, "bfloat16")
+for _n, _c in (("Ih", 128), ("P1", 128), ("P2", 128), ("S00", 128), ("S01", 128), ("S10", 128), ("S11", 128),
+               ("BO", 128), ("rg0", 16), ("rg1", 16), ("w16", 256), ("wd16", 256), ("x16", 256), ("Lm", 256), ("rcf", 256), ("a16", 256)):
+    _b(_n, _c, "float16")
+for _n, _c in (("ll", 96), ("l15", 16), ("colu", 16), ("off0", 16), ("zu", 16)):
+    _b(_n, _c, "uint16")
+for _t in range(1, TV + 1):
+    _b("X%d" % _t, 288, "bfloat16")
+    _b("SX%d" % _t, 288, "bfloat16")
+for _t in range(TV):
+    _b("Y%d" % _t, 256, "uint16")
+    _b("Z%d" % _t, 288, "bfloat16")
+    if _t:
+        _b("SY%d" % _t, 256, "uint16")
+        _b("SZ%d" % _t, 288, "bfloat16")
+for _n in ("PS0", "PS1", "PSD", "PST", "PSA", "PSL", "PSR", "PSF"):
+    _b(_n, 512, "float32", "psum")
+PSUM = ("PS0", "PS1", "PSD", "PST", "PSA", "PSL", "PSR", "PSF")
+
+SEMAPHORES = ["cv", "cs", "cp", "cg", "snt"] + ["d%d" % k for k in range(16)] + ["rx%d" % t for t in range(1, TV + 1)] + ["ry%d" % t for t in range(1, TV)] + ["rz%d" % t for t in range(1, TV)]
+
+
+def R(name, c0=0, c1=None, step=1, p0=0, p1=128):
+    buf, base, cols = TILE[name]
+    return (buf, base + c0, base + (cols if c1 is None else c1), step, p0, p1)
+
+
+def rank_program(g, core, T, topo):
+    rank = T.rank_of(core)
+    if rank is None:
+        return
+    n_ranks = len(T.cores)
+    dst = T.cores[(rank + 1) % n_ranks]
+    emask = topo.mask(core, dst)
+    neng = len(topo.engines(core, dst))
+    rid, pid, _se = topo.addr(dst)
+    Q = {"v": g.vector, "s": g.scalar, "p": g.tensor, "g": g, "y": g.sync}
+    SEMOF = {"v": "cv", "s": "cs", "p": "cp", "g": "cg"}
+    count = {}
+    known = {q: {} for q in Q}
+    snap = {}
+    log = {}
+    nd = [0]
+
+    def ap(r):
+        name, c0, c1, step, p0, p1 = r
+        if step == 1:
+            return T[name][p0:p1, c0:c1]
+        return T[name][p0:p1, c0:c1:step]
+
+    def wait(q, sem, val):
+        if known[q].get(sem, 0) >= val:
+            return
+        Q[q].wait_ge(T.sem[sem], val)
+        known[q][sem] = val
+        for s2, v2 in snap.get((sem, val), {}).items():
+            if known[q].get(s2, 0) < v2:
+                known[q][s2] = v2
+
+    def meet(a, b):
+        if a[4] >= b[5] or b[4] >= a[5] or a[1] >= b[2] or b[1] >= a[2]:
+            return False
+        return not (a[3] == b[3] and a[3] > 1 and (a[1] - b[1]) % a[3] != 0)
+
+    def covers(a, b):
+        return a[3] == 1 and a[4] <= b[4] and a[5] >= b[5] and a[1] <= b[1] and a[2] >= b[2]
+
+    def order(q, reads, writes, eng):
+        for r in reads:
+            ps = r[0] in PSUM
+            for (o, kind, sem, val, e) in log.get(r[0], []):
+                if ps:
+                    if (kind == "w" or e != eng) and not (e == eng == "p"):
+                        wait(q, sem, val)
+                elif kind == "w" and meet(r, o):
+                    wait(q, sem, val)
+        for r in writes:
+            ps = r[0] in PSUM
+            for (o, kind, sem, val, e) in log.get(r[0], []):
+                if ps:
+                    if e != eng:
+                        wait(q, sem, val)
+                elif meet(r, o) and (kind == "w" or e != eng):
+                    wait(q, sem, val)
+
+    def note(reads, writes, sem, val, eng):
+        for r in writes:
+            if r[0] in PSUM:
+                if any(e != eng for (_o, _k, _s, _v, e) in log.get(r[0], [])):
+                    log[r[0]] = []
+            old = [x for x in log.get(r[0], []) if not covers(r, x[0])]
+            log[r[0]] = old + [(r, "w", sem, val, eng)]
+        for r in reads:
+            old = [x for x in log.get(r[0], []) if not (x[1] == "r" and x[4] == eng and covers(r, x[0]))]
+            log[r[0]] = old + [(r, "r", sem, val, eng)]
+
+    def run(eng, fn, writes, reads):
+        order(eng, reads, writes, eng)
+        sem = SEMOF[eng]
+        val = count.get(sem, 0) + 1
+        count[sem] = val
+        snap[(sem, val)] = dict(known[eng])
+        fn().then_inc(T.sem[sem], 1)
+        note(reads, writes, sem, val, eng)
+
+    def dma(q, out, in_, writes, reads):
+        order(q, reads, writes, "d")
+        sem = "d%d" % nd[0]
+        nd[0] += 1
+        count[sem] = 16
+        snap[(sem, 16)] = dict(known[q])
+        Q[q].dma_start(out, in_).then_inc(T.sem[sem], 16)
+        note(reads, writes, sem, 16, sem)
+
+    def send(src, land, sem):
+        order("g", [src], [], "r")
+        count["snt"] = count.get("snt", 0) + neng
+        g.remote_dma(ap(land), ap(src), T.sem[sem], T.sem.snt, pid, rid, emask)
+        note([src], [], "snt", count["snt"], "r")
+        count[sem] = neng
+        note([], [land], sem, neng, sem)
+
+    def opnd(x):
+        if x[0] == "ind":
+            return ap(x[1]).indirect(ap(x[2])), [x[1], x[2]]
+        return ap(x), [x]
+
+    def ind(win, off):
+        return ("ind", win, off)
+
+    def tt(out, a, b, op):
+        (ia, ra), (ib, rb) = opnd(a), opnd(b)
+        run("v", lambda: g.vector.tensor_tensor(ap(out), ia, ib, op), [out], ra + rb)
+
+    def ts(out, a, s1, op0, s2=None, op1=None):
+        ia, ra = opnd(a)
+        rd = list(ra)
+        v1, v2 = s1, s2
+        if isinstance(s1, tuple):
+            v1 = ap(s1)
+            rd.append(s1)
+        if isinstance(s2, tuple):
+            v2 = ap(s2)
+            rd.append(s2)
+        if op1 is None:
+            run("v", lambda: g.vector.tensor_scalar(ap(out), ia, v1, None, op0), [out], rd)
+        else:
+            run("v", lambda: g.vector.tensor_scalar(ap(out), ia, v1, v2, op0, op1), [out], rd)
+
+    def cp(out, a):
+        (ia, ra), (io, ro) = opnd(a), opnd(out)
+        w = [out[1]] if out[0] == "ind" else [out]
+        run("v", lambda: g.vector.tensor_copy(io, ia), w, ra + ro[1:])
+
+    def ms(out, c):
+        run("v", lambda: g.vector.memset(ap(out), c), [out], [])
+
+    def scan(out, a, b, op0, op1):
+        run("v", lambda: g.vector.tensor_tensor_scan(ap(out), ap(a), ap(b), 0.0, op0, op1), [out], [a, b])
+
+    def vtr(out, a):
+        run("v", lambda: g.vector.transpose(ap(out), ap(a)), [out], [a])
+
+    def act(out, a, fn, bias=0.0, scale=1.0):
+        ia, ra = opnd(a)
+        sc = scale
+        rd = list(ra)
+        if isinstance(scale, tuple):
+            sc = ap(scale)
+            rd.append(scale)
+        run("s", lambda: g.scalar.activation(ap(out), ia, fn, bias=bias, scale=sc), [out], rd)
+
+    def mm(out, lhsT, rhs, start, stop):
+        run("p", lambda: g.tensor.matmul(ap(out), ap(lhsT), ap(rhs), start, stop), [out], [lhsT, rhs])
+
+    def iota(out, pattern, base, cm):
+        run("g", lambda: g.iota(ap(out), pattern, base, cm, allow_small_or_imprecise_dtypes=True), [out], [])
+
+    for q, tile, src in (("y", R("sdi", p1=8), T.sd[:]), ("y", R("nli", p1=8), T.nl[:]), ("y", R("wdi"), T.wd[:]), ("y", R("thi", 0, 1, p1=8), T.th[:]),
+                         ("y", R("wti", 0, 1), T.wt[:]), ("s", R("lsi"), T.ls[:]), ("s", R("xt", 0, 4096), T.x[:])):
+        dma(q, ap(tile), src, [tile], [])
+
+    iota(R("ioi"), [[1, 256]], 0, 0)
+    iota(R("pi", 0, 1), [[1, 1]], 0, 1)
+    iota(R("xi"), [[0, 16], [1, 16]], 0, 0)
+    iota(R("lli", 0, 64), [[-1, 4], [0, 2], [1, 8]], 8, 0)
+    iota(R("lli", 64, 96), [[-1, 2], [0, 2], [1, 8]], 8 - SIG[4], 0)
+    iota(R("llh"), [[0, 6], [8, 2], [0, 8]], 0, 0)
+    iota(R("g96", 0, 64), [[1, 4], [0, 2], [1, 8]], 0, 0)
+    iota(R("g96", 64, 96), [[1, 2], [0, 2], [1, 8]], SIG[4], 0)
+    iota(R("xt", 4096, 8192), [[0, 4096]], 0, 0)
+    iota(R("onf"), [[0, 128]], 1, 0)
+    iota(R("l15f", 0, 15), [[0, 15]], 0, 0)
+    for (h, j), k in POS.items():
+        if h < 8:
+            iota(R("l15f", k, k + 1), [[0, 1]], {4: 16, 2: 32, 1: 48}[h], 0)
+    for k, h in enumerate((1, 2, 4, 8)):
+        iota(R("mc", 16 * k, 16 * k + 16), [[0, 16]], 16 - h, 2 * h - 16)
+    iota(R("mc", 64, 80), [[0, 16]], 0, 0)
+    iota(R("Zp", 2048, 2064), [[0, 16]], 0, 0)
+    iota(R("zr"), [[0, 256], [16, 8]], 0, 0)
+
+    def pcol(k, p1=128):
+        return R("pc", k, k + 1, p1=p1)
+
+    def pint(k):
+        return R("pi", k, k + 1)
+    ts(pint(1), pint(0), 4, OP.arith_shift_right)
+    ts(pint(2), pint(0), 15, OP.bitwise_and)
+    ts(pint(3), pint(1), 1, OP.bitwise_and)
+    cp(R("pc", 0, 3), R("pi", 0, 3))
+    cp(pcol(6), pint(3))
+    cp(R("fi"), R("ioi", 0, 128))
+    ts(R("If"), R("fi"), pcol(0), OP.is_equal)
+    ts(R("lli"), R("lli"), 7, OP.bitwise_and)
+    tt(R("lli"), R("lli"), R("llh"), OP.add)
+    cp(R("ll"), R("lli"))
+    ts(R("mask"), R("xi"), pcol(2), OP.is_equal)
+    ts(pcol(3), pcol(1), 8.0, OP.add)
+    ts(R("rg0"), R("xi", 0, 16), pcol(1), OP.is_equal)
+    ts(R("rg1"), R("xi", 0, 16), pcol(3), OP.is_equal)
+    ts(R("I"), R("fi"), pcol(0), OP.is_equal)
+
+    B16 = R
+
+    def post(tn, Yd, Zd, fill):
+        LLt = R("ll", 16 * tn, 16 * tn + 16)
+        tt(B16("sq"), B16("sI"), B16("sI"), OP.mult)
+        ts(B16("sq5"), B16("sq"), 5, OP.arith_shift_right)
+        ts(B16("kI"), B16("nB"), 77.0, OP.mult)
+        tt(B16("w1"), B16("sq5"), B16("sI"), OP.add)
+        cp(R(Zd, 256, 272), B16("sI"))
+        tt(B16("cc"), B16("w1"), B16("kI"), OP.add)
+        ts(B16("cI"), B16("cc"), 2047, OP.bitwise_and)
+        tt(R(Zd, 272, 288), B16("sI"), R(Zd, 256, 272), OP.subtract)
+        tt(R("rcf"), ind(R("cI"), LLt), R("mask"), OP.mult)
+        tt(R("rq"), ind(R("rI"), LLt), R("xi"), OP.is_equal)
+        fill(0)
+        mm(R("PSL", 0, 16), R("rcf", 0, 128), R("rg0"), True, False)
+        mm(R("PSL", 0, 16), R("rcf", 128, 256), R("rg1"), False, True)
+        mm(R("PSR", 0, 128), R("rq", 0, 128), R("I"), True, True)
+        mm(R("PSR", 128, 256), R("rq", 128, 256), R("I"), True, True)
+        fill(1)
+        act(R(Zd, 0, 256), R("PSR", 0, 256), FN.Copy)
+        fill(2)
+        cp(R(Yd, 0, 16), R("PSL", 0, 16))
+        fill(3)
+
+    ts(pcol(7), pcol(6), -1.0, OP.mult, 1.0, OP.add)
+    ts(pcol(8), pcol(6), -32.0, OP.mult, 16.0, OP.add)
+    tt(pcol(8), pcol(8), pcol(0), OP.add)
+    ts(R("S00"), R("fi"), pcol(0), OP.is_equal, pcol(7), OP.mult)
+    ts(R("S11"), R("fi"), pcol(0), OP.is_equal, pcol(6), OP.mult)
+    ts(R("S01"), R("fi"), pcol(8), OP.is_equal, pcol(7), OP.mult)
+    ts(R("S10"), R("fi"), pcol(8), OP.is_equal, pcol(6), OP.mult)
+
+    cp(R("sdf", p1=8), R("sdi", p1=8))
+    cp(R("nlf", p1=8), R("nli", p1=8))
+    for h in range(2):
+        mm(R("PSA", 8 * h, 8 * h + 8), R("sdf", 128 * h, 128 * h + 128, p1=8), R("If", 0, 8, p1=8), True, True)
+        mm(R("PSA", 16 + 8 * h, 24 + 8 * h), R("nlf", 128 * h, 128 * h + 128, p1=8), R("If", 0, 8, p1=8), True, True)
+    cp(B16("sI"), R("PSA", 0, 16))
+    cp(B16("nB"), R("PSA", 16, 32))
+    ts(B16("rI"), B16("sI"), 15, OP.bitwise_and)
+    post(0, "Y0", "Z0", lambda k: None)
+    ts(R("wd16"), R("wdi"), -2048.0, OP.add)
+    vtr(R("x16"), R("wd16"))
+    for c in range(16):
+        b, c2 = c // 2, c % 2
+        o = R("PS0", c, 256, 16)
+        for g2 in range(2):
+            mm(o, R("S%d%d" % (c2, g2)), R("x16", 32 * b + 16 * g2, 32 * b + 16 * g2 + 16), g2 == 0, g2 == 1)
+    ts(R("gi", 0, 128), R("ioi", 0, 128), 4, OP.arith_shift_right)
+    ts(R("BO"), R("gi", 0, 128), pcol(1), OP.is_equal)
+    ts(R("d0s"), R("xi"), 0.0, OP.is_gt)
+    ts(R("g96"), R("g96"), 7, OP.bitwise_and)
+    ts(R("on"), R("g96"), pcol(1), OP.is_equal)
+    cp(pcol(11), R("wti", 0, 1))
+    act(R("NI"), R("I"), FN.Copy, scale=-1.0)
+    act(R("onm"), R("on"), FN.Copy, scale=-1.0)
+    act(R("I5"), R("I"), FN.Copy, scale=5.0)
+    act(R("wtb"), R("on"), FN.Copy, scale=pcol(11))
+    ts(R("Y0", 16, 256), R("PS0", 0, 240), 2048.0, OP.add)
+    ts(R("lsf"), R("lsi"), -2048.0, OP.add)
+
+    def later():
+        ts(R("l15", 0, 15), R("l15f", 0, 15), pcol(2), OP.add)
+        ts(pcol(10), pcol(2), 16.0, OP.mult)
+        ts(R("base"), R("ioi", 0, 16), 256.0, OP.mult, pcol(10), OP.add)
+        ts(R("zbase"), R("base"), 0.5, OP.mult, 15.0, OP.add)
+        cp(pcol(13, 8), R("thi", 0, 1, p1=8))
+        ts(R("thd", p1=8), R("g96", p1=8), pcol(0, 8), OP.is_equal, pcol(13, 8), OP.mult)
+        mm(R("PSA", 0, 96), R("onf", p1=8), R("thd", p1=8), True, True)
+        ts(pcol(14), pcol(0), 0.0, OP.is_equal, 131072.0, OP.mult)
+        ts(pcol(9), pcol(0), 1.0, OP.is_equal)
+        tt(pcol(9), pcol(9), pcol(14), OP.add)
+        ts(R("lc"), R("onf"), pcol(9), OP.mult)
+        ts(pint(4), pint(0), 16.0, OP.add)
+        ts(pint(5), pint(0), 32.0, OP.add)
+        ts(R("pi", 4, 6), R("pi", 4, 6), 127, OP.bitwise_and)
+        cp(R("pc", 4, 6), R("pi", 4, 6))
+        ts(R("thB"), R("PSA", 0, 96), 1.0, OP.add)
+        ts(R("rh0"), R("xi"), pcol(1), OP.is_equal)
+        ts(R("rh1"), R("xi"), pcol(3), OP.is_equal)
+        for name, k in (("P1", 4), ("P2", 5), ("Ih", 0)):
+            ts(R(name), R("fi"), pcol(k), OP.is_equal)
+        for name, k in (("N1", 4), ("N2", 5), ("N0", 0)):
+            ts(R(name), R("fi"), pcol(k), OP.is_equal, -4096.0, OP.mult)
+
+    def change(t):
+        X = "X%d" % t
+        tt(R("colf"), R(X, 256, 272), R("base"), OP.add)
+        cp(R("colu"), R("colf"))
+        tt(R("sm"), ind(R("xt"), R("colu")), R(X, 0, 256), OP.add)
+        ts(R("nv"), R("sm"), 0.5, OP.mult, -0.25, OP.add)
+        cp(ind(R("xt"), R("colu")), R("nv"))
+
+    for t in range(TV):
+        Y, Z = "Y%d" % t, "Z%d" % t
+        ont = R("on", 16 * t, 16 * t + 8)
+        wtt = R("wtb", 16 * t, 16 * t + 8)
+        LLt = R("ll", 16 * t, 16 * t + 16)
+
+        def row(j):
+            return R("G8", j, 2048, 8)
+
+        def off(j):
+            return R("off0") if j == 0 else R(Y, 16 * j, 16 * j + 16)
+
+        def gather(j):
+            act(row(j), ind(R("xt"), off(j)), FN.Copy)
+
+        def diff(k0, k1):
+            for k in range(k0, k1):
+                h, j = SHORT[k]
+                o = R("PS%d" % (k // 2 % 2), 256 * (k % 2), 256 * (k % 2) + 256)
+                mm(o, R("I"), row(j), True, False)
+                mm(o, R("NI"), row(j + h), False, True)
+
+        def absol(k0, k1):
+            act(R("ab", 256 * k0, 256 * k1), R("PS%d" % (k0 // 2 % 2), 0, 256 * (k1 - k0)), FN.Abs)
+
+        def dshort(k):
+            c = 16 * POS[SHORT[k]]
+            for h in range(2):
+                mm(R("PSD", c + 8 * h, c + 8 * h + 8), R("ab", 256 * k + 128 * h, 256 * k + 128 * h + 128), ont, True, True)
+
+        def long_(k):
+            j = LONG[k]
+            tt(R("d8", 256 * k, 256 * k + 256), ind(R("xt"), off(j + 8)), row(j), OP.subtract)
+
+        def absl(k0, k1):
+            act(R("r8", 256 * k0, 256 * k1), R("d8", 256 * k0, 256 * k1), FN.Abs)
+
+        def dlong(k):
+            c = 16 * POS[(8, LONG[k])]
+            for h in range(2):
+                a = 256 * k + 128 * h
+                o = R("PSD", c + 8 * h, c + 8 * h + 8)
+                if k >= 6:
+                    mm(o, R("d8", a, a + 128), R("onm", 16 * t, 16 * t + 8), True, False)
+                mm(o, R("r8", a, a + 128), ont, k < 6, True)
+
+        def limits():
+            ts(R("np1"), R("X%d" % t, 272, 288) if t else R("nB"), 1.0, OP.add, 16.0, OP.min)
+            for k, h in enumerate((8, 4, 2, 1)):
+                ts(R("en", 16 * k, 16 * k + 16), R("np1"), 2.0 * h, OP.is_ge)
+            for k in range(4):
+                tt(R("thr", 16 * k, 16 * k + 16), R("en", 16 * k, 16 * k + 16), R("B1") if t else R("thB", 0, 16), OP.mult)
+            cp(R("Bt"), ind(R("thr"), R("l15", 0, 15)))
+
+        if t:
+            change(t)
+            limits()
+        for j in (1, 3, 5, 7):
+            gather(j)
+        tt(R("Lm"), ind(R("lsf"), R(Y, 0, 16)), R(Z, 0, 256), OP.mult)
+        mm(R("PSF", 0, 256), R("BO"), R("Lm"), True, True)
+        diff(0, 2)
+        diff(2, 3)
+        ts(R("w16", 16, 256), R(Y, 16, 256), -2048.0, OP.add)
+        tt(R("dg"), R("PSF", 0, 256), R("mask"), OP.mult)
+        scan(R("lsc"), R("d0s"), R("dg"), OP.mult, OP.add)
+        ts(R("off0"), R("lsc", 15, 256, 16), 2048.0, OP.add)
+        cp(R("w16", 0, 16), R("lsc", 15, 256, 16))
+        long_(0)
+        long_(1)
+        if t == 0:
+            later()
+        gather(2)
+        absol(0, 2)
+        gather(6)
+        gather(0)
+        gather(4)
+        long_(2)
+        long_(3)
+        long_(4)
+        long_(5)
+        absl(0, 2)
+        dshort(0)
+        dshort(1)
+        diff(3, 4)
+        absol(2, 4)
+        diff(4, 6)
+        absol(4, 6)
+        absl(2, 4)
+        dlong(0)
+        dlong(1)
+        if t == 0:
+            limits()
+        scan(R("Zp", 0, 2048), R("zr"), R("G8"), OP.min, OP.max)
+        absl(4, 6)
+        tt(R("d8", 2048, 2304), ind(R("xt"), off(4)), row(0), OP.subtract)
+        act(R("ab", 1536, 1792), R("d8", 2048, 2304), FN.Abs)
+        long_(6)
+        long_(7)
+        ts(R("r8", 1536, 2048), R("d8", 1536, 2048), 0.0, OP.max, 2.0, OP.mult)
+        for k in (2, 3, 4, 5):
+            dshort(k)
+        dlong(2)
+        dlong(3)
+        PT = R("PST", 0, 80)
+        mm(PT, R("lc"), R("mc"), True, False)
+        mm(R("PST", 64, 80), R("I5"), R(Z, 256, 272), False, False)
+        mm(R("PST", 64, 80), R("I5"), R(Z, 272, 288), False, False)
+        for a, k in enumerate((1, 2, 4, 8, 1)):
+            for h in range(2):
+                mm(R("PST", 16 * a + 8 * h, 16 * a + 8 * h + 8), R("Zp", 1024 * h + k - 1, 1024 * h + 1024, 8), wtt, False, a == 4 and h == 1)
+        dshort(6)
+        for k in (4, 5, 6, 7):
+            dlong(k)
+        tt(R("good"), R("PSD", 0, 240), R("Bt"), OP.is_lt)
+        tt(R("m1"), R("good", 0, 112), R("good", 112, 224), OP.mult)
+        tt(R("u1"), R("PST", 0, 16), R("good", 224, 240), OP.mult)
+        tt(R("m2"), R("m1", 0, 48), R("m1", 48, 96), OP.mult)
+        tt(R("u2"), R("PST", 16, 32), R("m1", 96, 112), OP.mult)
+        tt(R("b8"), R("m2", 0, 16), R("m2", 16, 32), OP.mult)
+        tt(R("u3"), R("PST", 32, 48), R("m2", 32, 48), OP.mult)
+        tt(R("u4"), R("PST", 64, 80), R("u1"), OP.max)
+        tt(R("u5"), R("PST", 48, 64), R("b8"), OP.mult)
+        tt(R("u0"), R("u2"), R("u3"), OP.max)
+        tt(R("u6"), R("u4"), R("u5"), OP.max)
+        tt(R("vI"), R("u0"), R("u6"), OP.max)
+        ts(R("mI"), R("vI"), 17, OP.arith_shift_right)
+        ts(R("sI"), R("vI"), 4095, OP.bitwise_and)
+        tt(R("rh"), ind(R("mI"), LLt), R("mask"), OP.mult)
+        mm(R("PSF", 0, 16), R("rh", 0, 128), R("rh0", 0, 16), True, False)
+        mm(R("PSF", 0, 16), R("rh", 128, 256), R("rh1", 0, 16), False, True)
+        mm(R("PSA", 0, 256), R("rh", 0, 128), R("rh0"), True, False)
+        mm(R("PSA", 0, 256), R("rh", 128, 256), R("rh1"), False, True)
+        ts(R("M4"), R("mI"), 1.0, OP.is_lt, 4096.0, OP.mult)
+        ts(R("rI"), R("sI"), 15, OP.bitwise_and)
+        tt(R("loI"), R("rI"), R("M4"), OP.max)
+        tt(R("zf"), R("zbase"), R("PSF", 0, 16), OP.subtract)
+        ts(R("hJ"), R("mI"), -1.0, OP.mult, 16.0, OP.add)
+        cp(R("zu"), R("zf"))
+        tt(R("rl"), ind(R("loI"), LLt), R("mask"), OP.mult)
+        ts(R("hI"), R("hJ"), 15, OP.bitwise_and)
+        mm(R("PSL", 0, 16), R("rl", 0, 128), R("rh0", 0, 16), True, False)
+        mm(R("PSL", 0, 16), R("rl", 128, 256), R("rh1", 0, 16), False, True)
+        SX = "SX%d" % (t + 1)
+        act(R(SX, 0, 256), ind(R("Zp"), R("zu")), FN.Copy)
+        tt(R("nB"), R("np1"), R("hI"), OP.subtract)
+        tt(R(SX, 272, 288), R("np1"), R("hI"), OP.subtract)
+        cp(R(SX, 256, 272), R("PSL", 0, 16))
+        send(R(SX), R("X%d" % (t + 1)), "rx%d" % (t + 1))
+
+        last = t == TV - 1
+        step = 0 if last else SIG[t + 1] - SIG[t]
+        HI, LO = R("P%d" % step) if step else R("Ih"), R("N%d" % step)
+        full = 256 if last else 240
+
+        def width(h):
+            return min(full, 256 - 16 * h)
+
+        def pen(h):
+            act(R("pen%d" % h, 0, width(h)), R("PSA", 0, width(h)), FN.Abs, float(h - 16 if h else 0))
+
+        def close_pe(k, h):
+            o, n = R(CB[k], 0, width(h)), width(h)
+            mm(o, HI, R("w16", 16 * h, 16 * h + n), True, False)
+            mm(o, LO, R("pen%d" % h, 0, n), False, True)
+
+        def close_v(k, h):
+            n = width(h)
+            if k == 0:
+                ts(R("acc", 0, n), R("PS0", 0, n), -2048.0, OP.max)
+            else:
+                tt(R("acc", 0, n), R(CB[k], 0, n), R("acc", 0, n), OP.max)
+
+        HS = (0, 1, 2, 4, 8)
+        CB = ("PS0", "PS1", "PSD", "PST", "PS0")
+        for h in HS:
+            pen(h)
+        if not last:
+            def fill(k):
+                if k == 0:
+                    close_pe(0, 0)
+                    close_pe(1, 1)
+                    close_pe(2, 2)
+                    close_pe(3, 4)
+                    close_v(0, 0)
+                    run("v", lambda: g.vector.tensor_reduce(ap(R("cnt", 0, 1)), ap(R("M4")), AxisListType.X, OP.add), [R("cnt", 0, 1)], [R("M4")])
+                elif k == 1:
+                    close_pe(4, 8)
+                    mm(R("PSF", 0, 1), R("onf"), R("cnt", 0, 1), True, True)
+                elif k == 2:
+                    send(R("SZ%d" % (t + 1)), R("Z%d" % (t + 1)), "rz%d" % (t + 1))
+                    close_v(1, 1)
+                    close_v(2, 2)
+                    close_v(3, 4)
+                    close_v(4, 8)
+                    ts(R("SY%d" % (t + 1), 16, 256), R("acc", 0, 240), 2048.0, OP.add)
+                else:
+                    send(R("SY%d" % (t + 1)), R("Y%d" % (t + 1)), "ry%d" % (t + 1))
+                    ts(R("amI", 0, 1), R("PSF", 0, 1), -1.0 / 4096, OP.mult, 2048.0, OP.add)
+                    ts(R("amJ", 0, 1), R("amI", 0, 1), 15, OP.bitwise_and)
+                    cp(R("amc", 1, 2), R("amJ", 0, 1))
+                    ts(R("B1"), R("thB", 16 * t + 16, 16 * t + 32), R("amc", 1, 2), OP.add)
+            post(t + 1, "SY%d" % (t + 1), "SZ%d" % (t + 1), fill)
+        else:
+            for k, h in enumerate(HS):
+                close_pe(k, h)
+                close_v(k, h)
+            cp(R("sfo"), R("sI"))
+            cp(R("a16"), R("acc"))
+            for h in range(2):
+                mm(R("PSF", 128 * h, 128 * h + 128, p1=8), R("nB", 8 * h, 8 * h + 8), R("If"), True, True)
+                mm(R("PSF", 256 + 128 * h, 384 + 128 * h, p1=8), R("sfo", 8 * h, 8 * h + 8), R("If"), True, True)
+            for b in range(8):
+                for g2 in range(2):
+                    o = R("PSR", 32 * b + 16 * g2, 32 * b + 16 * g2 + 16)
+                    for c2 in range(2):
+                        mm(o, R("S%d%d" % (g2, c2)), R("a16", 2 * b + c2, 256, 16), c2 == 0, c2 == 1)
+            act(R("yns", p1=8), R("PSF", p1=8), FN.Copy)
+            act(R("ywx"), R("PSR", 0, 256), FN.Copy, bias=2048.0)
+            change(TV)
+            dma("y", T.yx[:], T.xt[:, 0:4096], [], [R("xt", 0, 4096)])
+            vtr(R("yws"), R("ywx"))
+            k = 8 - SIG[t]
+            for y, c0 in ((T.yn, 0), (T.ys, 256)):
+                for b0, b1, g0, g1 in ((SIG[t], 8, 0, k), (0, SIG[t], k, 8)):
+                    r = R("yns", c0, c0 + 256, p0=g0, p1=g1)
+                    dma("s", y[b0:b1, :], ap(r), [], [r])
+            dma("y", T.yw[:], ap(R("yws")), [], [R("yws")])
+    for sem in SEMAPHORES:
+        if count.get(sem, 0):
+            wait("g", sem, count[sem])

@@ -17,7 +17,7 @@ _USED = {k: 0 for k in _ARENA}
 
 
 def _b(name, cols, dtype, where="sbuf"):
-    if where == "sbuf" and name[0] not in "XYZ" and name[:2] not in ("SX", "SY", "SZ") and name != "xt":
+    if where == "sbuf" and name[0] not in "XYZC" and name[:2] not in ("SX", "SY", "SZ", "SC") and name != "xt":
         TILE[name] = (_ARENA[dtype], _USED[dtype], cols)
         _USED[dtype] += (cols + 15) // 16 * 16
         SCRATCH[_ARENA[dtype]] = ("sbuf", [128, _USED[dtype]], dtype)
@@ -27,23 +27,23 @@ def _b(name, cols, dtype, where="sbuf"):
 
 
 for _n, _c in (("lsi", 2048), ("wdi", 256), ("sdi", 256), ("nli", 256), ("thi", 8), ("wti", 8), ("ioi", 256), ("pi", 16), ("gi", 256),
-               ("g96", 96), ("lli", 96), ("llh", 96), ("vI", 16), ("hI", 16), ("hJ", 16), ("mI", 16), ("sI", 16), ("rI", 16), ("loI", 16), ("sq", 16), ("sq5", 16), ("w1", 16),
+               ("g96", 96), ("lli", 96), ("llh", 96), ("vI", 16), ("hI", 16), ("hJ", 16), ("mI", 16), ("sI", 16), ("rI", 16), ("q16", 16), ("pk", 16), ("pI", 16), ("mA", 16), ("rA", 16), ("sq", 16), ("sq5", 16), ("w1", 16),
                ("kI", 16), ("cc", 16), ("cI", 16), ("nv", 256), ("amI", 8), ("amJ", 8), ("xii", 256)):
     _b(_n, _c, "int32")
 for _n, _c in (("lsf", 2048), ("sdf", 256), ("nlf", 256), ("pc", 32), ("xi", 256), ("fi", 128), ("If", 128), ("onf", 128),
                ("thd", 96), ("thB", 96), ("base", 16), ("zbase", 16), ("d0s", 256), ("l15f", 16),
                ("colf", 16), ("dg", 256), ("lsc", 256), ("np1", 16), ("en", 64), ("thr", 64), ("B1", 16), ("Bt", 240), ("amc", 8),
-               ("u0", 16), ("u1", 16), ("u2", 16), ("u3", 16), ("u4", 16), ("u5", 16), ("u6", 16),
+               ("gif", 128), ("gd", 128), ("ge", 128), ("BOf", 128), ("Lmf", 256), ("u0", 16), ("u1", 16), ("u2", 16), ("u3", 16), ("u4", 16), ("u5", 16), ("u6", 16),
                ("zf", 16), ("M4", 16), ("cnt", 8), ("nB", 16), ("acc", 256), ("sfo", 16), ("ywx", 256), ("yws", 256), ("yns", 512)):
     _b(_n, _c, "float32")
-for _n, _c in (("xt", 8192), ("I", 128), ("NI", 128), ("I5", 128), ("rh0", 256), ("rh1", 256), ("mask", 256), ("zr", 2048), ("mc", 80), ("lc", 128), ("on", 96), ("onm", 96),
+for _n, _c in (("xt", 8192), ("I", 128), ("NI", 128), ("I5", 128), ("rB", 16), ("rd", 256), ("rh0", 16), ("rh1", 16), ("mB", 16), ("mrep", 256), ("mask", 256), ("zr", 2048), ("mc", 80), ("lc", 128), ("on", 96), ("onm", 96),
                ("wtb", 96), ("G8", 2048), ("Zp", 2064), ("d8", 2304), ("r8", 2048),
                ("pen0", 256), ("pen1", 256), ("pen2", 256), ("pen4", 256), ("pen8", 256), ("N0", 128), ("N1", 128), ("N2", 128), ("ab", 1792), ("sm", 256), ("good", 240), ("m1", 112), ("m2", 48), ("b8", 16), ("rh", 256), ("rl", 256), ("rq", 256)):
     _b(_n, _c, "bfloat16")
 for _n, _c in (("Ih", 128), ("P1", 128), ("P2", 128), ("S00", 128), ("S01", 128), ("S10", 128), ("S11", 128),
                ("BO", 128), ("rg0", 16), ("rg1", 16), ("w16", 256), ("wd16", 256), ("x16", 256), ("Lm", 256), ("rcf", 256), ("a16", 256)):
     _b(_n, _c, "float16")
-for _n, _c in (("ll", 96), ("l15", 16), ("colu", 16), ("off0", 16), ("zu", 16)):
+for _n, _c in (("ll", 96), ("l15", 16), ("l16", 16), ("colu", 16), ("colv", 8), ("off0", 16), ("zu", 16)):
     _b(_n, _c, "uint16")
 for _t in range(1, TV + 1):
     _b("X%d" % _t, 288, "bfloat16")
@@ -209,7 +209,11 @@ def rank_program(g, core, T, topo):
         if isinstance(scale, tuple):
             sc = ap(scale)
             rd.append(scale)
-        run("s", lambda: g.scalar.activation(ap(out), ia, fn, bias=bias, scale=sc), [out], rd)
+        bi = bias
+        if isinstance(bias, tuple):
+            bi = ap(bias)
+            rd.append(bias)
+        run("s", lambda: g.scalar.activation(ap(out), ia, fn, bias=bi, scale=sc), [out], rd)
 
     def mm(out, lhsT, rhs, start, stop):
         run("p", lambda: g.tensor.matmul(ap(out), ap(lhsT), ap(rhs), start, stop), [out], [lhsT, rhs])
@@ -217,8 +221,8 @@ def rank_program(g, core, T, topo):
     def iota(out, pattern, base, cm):
         run("g", lambda: g.iota(ap(out), pattern, base, cm, allow_small_or_imprecise_dtypes=True), [out], [])
 
-    for q, tile, src in (("y", R("sdi", p1=8), T.sd[:]), ("y", R("nli", p1=8), T.nl[:]), ("y", R("wdi"), T.wd[:]), ("y", R("thi", 0, 1, p1=8), T.th[:]),
-                         ("y", R("wti", 0, 1), T.wt[:]), ("s", R("lsi"), T.ls[:]), ("s", R("xt", 0, 4096), T.x[:])):
+    for q, tile, src in (("y", R("sdi", p1=8), T.sd[:]), ("s", R("sdi", p0=8, p1=16), T.nl[:]), ("y", R("wdi"), T.wd[:]), ("s", R("xt", 0, 4096), T.x[:]),
+                         ("s", R("lsi"), T.ls[:]), ("y", R("thi", 0, 1, p1=8), T.th[:]), ("y", R("wti", 0, 1), T.wt[:])):
         dma(q, ap(tile), src, [tile], [])
 
     iota(R("ioi"), [[1, 256]], 0, 0)
@@ -229,7 +233,7 @@ def rank_program(g, core, T, topo):
     iota(R("llh"), [[0, 6], [8, 2], [0, 8]], 0, 0)
     iota(R("g96", 0, 64), [[1, 4], [0, 2], [1, 8]], 0, 0)
     iota(R("g96", 64, 96), [[1, 2], [0, 2], [1, 8]], SIG[4], 0)
-    iota(R("xt", 4096, 8192), [[0, 4096]], 0, 0)
+    iota(R("gif"), [[1, 8], [0, 16]], 0, 0)
     iota(R("onf"), [[0, 128]], 1, 0)
     iota(R("l15f", 0, 15), [[0, 15]], 0, 0)
     for (h, j), k in POS.items():
@@ -239,6 +243,9 @@ def rank_program(g, core, T, topo):
         iota(R("mc", 16 * k, 16 * k + 16), [[0, 16]], 16 - h, 2 * h - 16)
     iota(R("mc", 64, 80), [[0, 16]], 0, 0)
     iota(R("Zp", 2048, 2064), [[0, 16]], 0, 0)
+    iota(R("xt", 6144, 8192), [[0, 2048]], 0, 0)
+    for k in range(8):
+        act(R("xt", 4096 + 256 * k, 4352 + 256 * k), R("xi"), FN.Copy, scale=0.0)
     iota(R("zr"), [[0, 256], [16, 8]], 0, 0)
 
     def pcol(k, p1=128):
@@ -250,9 +257,10 @@ def rank_program(g, core, T, topo):
     ts(pint(2), pint(0), 15, OP.bitwise_and)
     ts(pint(3), pint(1), 1, OP.bitwise_and)
     cp(R("pc", 0, 3), R("pi", 0, 3))
-    cp(pcol(6), pint(3))
     cp(R("fi"), R("ioi", 0, 128))
     ts(R("If"), R("fi"), pcol(0), OP.is_equal)
+    cp(pcol(6), pint(3))
+    ts(pcol(15), pcol(2), -1.0, OP.mult)
     ts(R("lli"), R("lli"), 7, OP.bitwise_and)
     tt(R("lli"), R("lli"), R("llh"), OP.add)
     cp(R("ll"), R("lli"))
@@ -260,33 +268,43 @@ def rank_program(g, core, T, topo):
     ts(pcol(3), pcol(1), 8.0, OP.add)
     ts(R("rg0"), R("xi", 0, 16), pcol(1), OP.is_equal)
     ts(R("rg1"), R("xi", 0, 16), pcol(3), OP.is_equal)
-    ts(R("I"), R("fi"), pcol(0), OP.is_equal)
+    ts(pcol(16), pcol(1), -1.0, OP.mult)
 
     B16 = R
 
-    def post(tn, Yd, Zd, fill):
+    def post(tn, Yd, Zd, n_at, fill):
         LLt = R("ll", 16 * tn, 16 * tn + 16)
         tt(B16("sq"), B16("sI"), B16("sI"), OP.mult)
         ts(B16("sq5"), B16("sq"), 5, OP.arith_shift_right)
-        ts(B16("kI"), B16("nB"), 77.0, OP.mult)
+        ts(B16("kI"), n_at, 77.0, OP.mult)
+        cp(B16("rB"), B16("rI"))
         tt(B16("w1"), B16("sq5"), B16("sI"), OP.add)
         cp(R(Zd, 256, 272), B16("sI"))
         tt(B16("cc"), B16("w1"), B16("kI"), OP.add)
         ts(B16("cI"), B16("cc"), 2047, OP.bitwise_and)
         tt(R(Zd, 272, 288), B16("sI"), R(Zd, 256, 272), OP.subtract)
         tt(R("rcf"), ind(R("cI"), LLt), R("mask"), OP.mult)
-        tt(R("rq"), ind(R("rI"), LLt), R("xi"), OP.is_equal)
         fill(0)
-        mm(R("PSL", 0, 16), R("rcf", 0, 128), R("rg0"), True, False)
-        mm(R("PSL", 0, 16), R("rcf", 128, 256), R("rg1"), False, True)
-        mm(R("PSR", 0, 128), R("rq", 0, 128), R("I"), True, True)
-        mm(R("PSR", 128, 256), R("rq", 128, 256), R("I"), True, True)
+        mm(R("PSF", 0, 16), R("rcf", 0, 128), R("rg0"), True, False)
+        mm(R("PSF", 0, 16), R("rcf", 128, 256), R("rg1"), False, True)
         fill(1)
-        act(R(Zd, 0, 256), R("PSR", 0, 256), FN.Copy)
+        cp(R(Yd, 240, 256), R("PSF", 0, 16))
         fill(2)
-        cp(R(Yd, 0, 16), R("PSL", 0, 16))
+        act(R("rq"), ind(R("rB"), LLt), FN.Copy)
+        mm(R("PST", 0, 128), R("rq", 0, 128), R("I"), True, True)
+        mm(R("PST", 128, 256), R("rq", 128, 256), R("I"), True, True)
+        act(R("rd"), R("PST", 0, 256), FN.Abs, bias=pcol(15))
+        act(R(Zd, 0, 256), R("rd"), FN.Relu, bias=1.0, scale=-1.0)
         fill(3)
 
+    cp(R("sdf", p1=16), R("sdi", p1=16))
+    for h in range(2):
+        for k in range(2):
+            mm(R("PSA", 16 * k + 8 * h, 16 * k + 8 * h + 8), R("sdf", 128 * h, 128 * h + 128, p1=16), R("If", 8 * k, 8 * k + 8, p1=16), True, True)
+    act(R("I"), R("If"), FN.Copy)
+    act(R("d0s"), R("xi"), FN.Sign)
+    act(R("gd"), R("gif"), FN.Abs, bias=pcol(16))
+    act(R("BOf"), R("gd"), FN.Relu, bias=1.0, scale=-1.0)
     ts(pcol(7), pcol(6), -1.0, OP.mult, 1.0, OP.add)
     ts(pcol(8), pcol(6), -32.0, OP.mult, 16.0, OP.add)
     tt(pcol(8), pcol(8), pcol(0), OP.add)
@@ -294,16 +312,10 @@ def rank_program(g, core, T, topo):
     ts(R("S11"), R("fi"), pcol(0), OP.is_equal, pcol(6), OP.mult)
     ts(R("S01"), R("fi"), pcol(8), OP.is_equal, pcol(7), OP.mult)
     ts(R("S10"), R("fi"), pcol(8), OP.is_equal, pcol(6), OP.mult)
-
-    cp(R("sdf", p1=8), R("sdi", p1=8))
-    cp(R("nlf", p1=8), R("nli", p1=8))
-    for h in range(2):
-        mm(R("PSA", 8 * h, 8 * h + 8), R("sdf", 128 * h, 128 * h + 128, p1=8), R("If", 0, 8, p1=8), True, True)
-        mm(R("PSA", 16 + 8 * h, 24 + 8 * h), R("nlf", 128 * h, 128 * h + 128, p1=8), R("If", 0, 8, p1=8), True, True)
     cp(B16("sI"), R("PSA", 0, 16))
     cp(B16("nB"), R("PSA", 16, 32))
     ts(B16("rI"), B16("sI"), 15, OP.bitwise_and)
-    post(0, "Y0", "Z0", lambda k: None)
+    post(0, "Y0", "Z0", R("nB"), lambda k: None)
     ts(R("wd16"), R("wdi"), -2048.0, OP.add)
     vtr(R("x16"), R("wd16"))
     for c in range(16):
@@ -311,9 +323,6 @@ def rank_program(g, core, T, topo):
         o = R("PS0", c, 256, 16)
         for g2 in range(2):
             mm(o, R("S%d%d" % (c2, g2)), R("x16", 32 * b + 16 * g2, 32 * b + 16 * g2 + 16), g2 == 0, g2 == 1)
-    ts(R("gi", 0, 128), R("ioi", 0, 128), 4, OP.arith_shift_right)
-    ts(R("BO"), R("gi", 0, 128), pcol(1), OP.is_equal)
-    ts(R("d0s"), R("xi"), 0.0, OP.is_gt)
     ts(R("g96"), R("g96"), 7, OP.bitwise_and)
     ts(R("on"), R("g96"), pcol(1), OP.is_equal)
     cp(pcol(11), R("wti", 0, 1))
@@ -321,14 +330,13 @@ def rank_program(g, core, T, topo):
     act(R("onm"), R("on"), FN.Copy, scale=-1.0)
     act(R("I5"), R("I"), FN.Copy, scale=5.0)
     act(R("wtb"), R("on"), FN.Copy, scale=pcol(11))
-    ts(R("Y0", 16, 256), R("PS0", 0, 240), 2048.0, OP.add)
-    ts(R("lsf"), R("lsi"), -2048.0, OP.add)
 
     def later():
         ts(R("l15", 0, 15), R("l15f", 0, 15), pcol(2), OP.add)
+        ts(R("l16"), R("xi", 0, 16), 0.0, OP.mult, pcol(2), OP.add)
         ts(pcol(10), pcol(2), 16.0, OP.mult)
         ts(R("base"), R("ioi", 0, 16), 256.0, OP.mult, pcol(10), OP.add)
-        ts(R("zbase"), R("base"), 0.5, OP.mult, 15.0, OP.add)
+        ts(R("zbase"), R("base"), 8.0, OP.mult, 247.5, OP.add)
         cp(pcol(13, 8), R("thi", 0, 1, p1=8))
         ts(R("thd", p1=8), R("g96", p1=8), pcol(0, 8), OP.is_equal, pcol(13, 8), OP.mult)
         mm(R("PSA", 0, 96), R("onf", p1=8), R("thd", p1=8), True, True)
@@ -340,13 +348,27 @@ def rank_program(g, core, T, topo):
         ts(pint(5), pint(0), 32.0, OP.add)
         ts(R("pi", 4, 6), R("pi", 4, 6), 127, OP.bitwise_and)
         cp(R("pc", 4, 6), R("pi", 4, 6))
-        ts(R("thB"), R("PSA", 0, 96), 1.0, OP.add)
-        ts(R("rh0"), R("xi"), pcol(1), OP.is_equal)
-        ts(R("rh1"), R("xi"), pcol(3), OP.is_equal)
+        ts(R("rh0"), R("xi", 0, 16), pcol(1), OP.is_equal)
+        ts(R("rh1"), R("xi", 0, 16), pcol(3), OP.is_equal)
         for name, k in (("P1", 4), ("P2", 5), ("Ih", 0)):
             ts(R(name), R("fi"), pcol(k), OP.is_equal)
-        for name, k in (("N1", 4), ("N2", 5), ("N0", 0)):
-            ts(R(name), R("fi"), pcol(k), OP.is_equal, -4096.0, OP.mult)
+        ts(R("BO"), R("gif"), pcol(1), OP.is_equal)
+        ts(R("thB"), R("PSA", 0, 96), 1.0, OP.add)
+        ts(R("pc", 17, 19), R("pc", 4, 6), -1.0, OP.mult)
+
+    def negated():
+        for name, k in (("N1", 17), ("N2", 18)):
+            act(R("gd"), R("fi"), FN.Abs, bias=pcol(k))
+            act(R("ge"), R("gd"), FN.Relu, bias=1.0, scale=-1.0)
+            act(R(name), R("ge"), FN.Copy, scale=-4096.0)
+        act(R("N0"), R("If"), FN.Copy, scale=-4096.0)
+
+    def table(k):
+        ts(R("lsf", 512 * k, 512 * k + 512), R("lsi", 512 * k, 512 * k + 512), -2048.0, OP.add)
+
+    later()
+    ts(R("Y0", 0, 240), R("PS0", 0, 240), 2048.0, OP.add)
+    ts(R("thB"), R("PSA", 0, 96), 1.0, OP.add)
 
     def change(t):
         X = "X%d" % t
@@ -366,7 +388,7 @@ def rank_program(g, core, T, topo):
             return R("G8", j, 2048, 8)
 
         def off(j):
-            return R("off0") if j == 0 else R(Y, 16 * j, 16 * j + 16)
+            return R("off0") if j == 0 else R(Y, 16 * j - 16, 16 * j)
 
         def gather(j):
             act(row(j), ind(R("xt"), off(j)), FN.Copy)
@@ -398,37 +420,43 @@ def rank_program(g, core, T, topo):
             for h in range(2):
                 a = 256 * k + 128 * h
                 o = R("PSD", c + 8 * h, c + 8 * h + 8)
-                if k >= 6:
+                if k >= 4:
                     mm(o, R("d8", a, a + 128), R("onm", 16 * t, 16 * t + 8), True, False)
-                mm(o, R("r8", a, a + 128), ont, k < 6, True)
+                mm(o, R("r8", a, a + 128), ont, k < 4, True)
 
         def limits():
-            ts(R("np1"), R("X%d" % t, 272, 288) if t else R("nB"), 1.0, OP.add, 16.0, OP.min)
+            n_in = R("X%d" % t, 272, 288) if t else R("nB")
             for k, h in enumerate((8, 4, 2, 1)):
-                ts(R("en", 16 * k, 16 * k + 16), R("np1"), 2.0 * h, OP.is_ge)
+                act(R("en", 16 * k, 16 * k + 16), n_in, FN.Sign, bias=1.5 - 2 * h)
+            ts(R("np1"), n_in, 1.0, OP.add, 16.0, OP.min)
             for k in range(4):
                 tt(R("thr", 16 * k, 16 * k + 16), R("en", 16 * k, 16 * k + 16), R("B1") if t else R("thB", 0, 16), OP.mult)
-            cp(R("Bt"), ind(R("thr"), R("l15", 0, 15)))
 
         if t:
             change(t)
-            limits()
+        limits()
         for j in (1, 3, 5, 7):
             gather(j)
-        tt(R("Lm"), ind(R("lsf"), R(Y, 0, 16)), R(Z, 0, 256), OP.mult)
-        mm(R("PSF", 0, 256), R("BO"), R("Lm"), True, True)
-        diff(0, 2)
+        gather(2)
+        ts(R("w16", 16, 256), R(Y, 0, 240), -2048.0, OP.add)
+        long_(0)
+        diff(0, 1)
+        if t:
+            tt(R("Lm"), ind(R("lsf"), R(Y, 240, 256)), R(Z, 0, 256), OP.mult)
+            mm(R("PSF", 0, 256), R("BO"), R("Lm"), True, True)
+        else:
+            tt(R("Lmf"), ind(R("lsi"), R(Y, 240, 256)), R(Z, 0, 256), OP.mult)
+            mm(R("PSF", 0, 256), R("BOf"), R("Lmf"), True, True)
+        diff(1, 2)
         diff(2, 3)
-        ts(R("w16", 16, 256), R(Y, 16, 256), -2048.0, OP.add)
+        mm(R("PST", 0, 80), R("lc"), R("mc"), True, False)
+        mm(R("PST", 64, 80), R("I5"), R(Z, 256, 272), False, False)
+        mm(R("PST", 64, 80), R("I5"), R(Z, 272, 288), False, False)
+        long_(1)
         tt(R("dg"), R("PSF", 0, 256), R("mask"), OP.mult)
         scan(R("lsc"), R("d0s"), R("dg"), OP.mult, OP.add)
-        ts(R("off0"), R("lsc", 15, 256, 16), 2048.0, OP.add)
-        cp(R("w16", 0, 16), R("lsc", 15, 256, 16))
-        long_(0)
-        long_(1)
-        if t == 0:
-            later()
-        gather(2)
+        ts(R("off0"), R("lsc", 15, 256, 16), 2048.0 if t else 0.0, OP.add)
+        ts(R("w16", 0, 16), R("lsc", 15, 256, 16), 0.0 if t else -2048.0, OP.add)
         absol(0, 2)
         gather(6)
         gather(0)
@@ -437,39 +465,55 @@ def rank_program(g, core, T, topo):
         long_(3)
         long_(4)
         long_(5)
-        absl(0, 2)
+        diff(3, 4)
         dshort(0)
         dshort(1)
-        diff(3, 4)
         absol(2, 4)
+        absl(0, 2)
         diff(4, 6)
-        absol(4, 6)
-        absl(2, 4)
         dlong(0)
         dlong(1)
-        if t == 0:
-            limits()
+        dshort(2)
+        dshort(3)
+        absol(4, 6)
+        absl(2, 4)
         scan(R("Zp", 0, 2048), R("zr"), R("G8"), OP.min, OP.max)
-        absl(4, 6)
         tt(R("d8", 2048, 2304), ind(R("xt"), off(4)), row(0), OP.subtract)
         act(R("ab", 1536, 1792), R("d8", 2048, 2304), FN.Abs)
+        ts(R("r8", 1024, 1536), R("d8", 1024, 1536), 0.0, OP.max, 2.0, OP.mult)
         long_(6)
         long_(7)
         ts(R("r8", 1536, 2048), R("d8", 1536, 2048), 0.0, OP.max, 2.0, OP.mult)
-        for k in (2, 3, 4, 5):
-            dshort(k)
+        act(R("Bt"), ind(R("thr"), R("l15", 0, 15)), FN.Copy)
+
+        def terms(blocks):
+            for a, k in blocks:
+                for h in range(2):
+                    mm(R("PST", 16 * a + 8 * h, 16 * a + 8 * h + 8), R("Zp", 1024 * h + k - 1, 1024 * h + 1024, 8), wtt, False, a == 3 and h == 1)
+        dshort(4)
+        dshort(5)
+        terms(((0, 1), (4, 1), (1, 2)))
         dlong(2)
         dlong(3)
-        PT = R("PST", 0, 80)
-        mm(PT, R("lc"), R("mc"), True, False)
-        mm(R("PST", 64, 80), R("I5"), R(Z, 256, 272), False, False)
-        mm(R("PST", 64, 80), R("I5"), R(Z, 272, 288), False, False)
-        for a, k in enumerate((1, 2, 4, 8, 1)):
-            for h in range(2):
-                mm(R("PST", 16 * a + 8 * h, 16 * a + 8 * h + 8), R("Zp", 1024 * h + k - 1, 1024 * h + 1024, 8), wtt, False, a == 4 and h == 1)
+        dlong(4)
+        dlong(5)
         dshort(6)
-        for k in (4, 5, 6, 7):
-            dlong(k)
+        dlong(6)
+        dlong(7)
+        terms(((2, 4), (3, 8)))
+        last = t == TV - 1
+        step = 0 if last else SIG[t + 1] - SIG[t]
+        HI, LO = R("P%d" % step) if step else R("Ih"), R("N%d" % step)
+        full = 256 if last else 240
+        HS = (0, 1, 2, 4, 8)
+        CB = ("PS0", "PS1", "PSA", "PSL", "PSR")
+        for k, h in enumerate(HS):
+            n = min(full, 256 - 16 * h)
+            mm(R(CB[k], 0, n), HI, R("w16", 16 * h, 16 * h + n), True, False)
+        if t == 0:
+            negated()
+            table(0)
+            table(1)
         tt(R("good"), R("PSD", 0, 240), R("Bt"), OP.is_lt)
         tt(R("m1"), R("good", 0, 112), R("good", 112, 224), OP.mult)
         tt(R("u1"), R("PST", 0, 16), R("good", 224, 240), OP.mult)
@@ -482,45 +526,38 @@ def rank_program(g, core, T, topo):
         tt(R("u0"), R("u2"), R("u3"), OP.max)
         tt(R("u6"), R("u4"), R("u5"), OP.max)
         tt(R("vI"), R("u0"), R("u6"), OP.max)
+        ts(R("q16"), R("vI"), 13, OP.arith_shift_right, 240, OP.bitwise_and)
+        ts(R("rI"), R("vI"), 15, OP.bitwise_and)
         ts(R("mI"), R("vI"), 17, OP.arith_shift_right)
-        ts(R("sI"), R("vI"), 4095, OP.bitwise_and)
-        tt(R("rh"), ind(R("mI"), LLt), R("mask"), OP.mult)
-        mm(R("PSF", 0, 16), R("rh", 0, 128), R("rh0", 0, 16), True, False)
-        mm(R("PSF", 0, 16), R("rh", 128, 256), R("rh1", 0, 16), False, True)
-        mm(R("PSA", 0, 256), R("rh", 0, 128), R("rh0"), True, False)
-        mm(R("PSA", 0, 256), R("rh", 128, 256), R("rh1"), False, True)
-        ts(R("M4"), R("mI"), 1.0, OP.is_lt, 4096.0, OP.mult)
-        ts(R("rI"), R("sI"), 15, OP.bitwise_and)
-        tt(R("loI"), R("rI"), R("M4"), OP.max)
-        tt(R("zf"), R("zbase"), R("PSF", 0, 16), OP.subtract)
+        tt(R("pk"), R("q16"), R("rI"), OP.add)
         ts(R("hJ"), R("mI"), -1.0, OP.mult, 16.0, OP.add)
-        cp(R("zu"), R("zf"))
-        tt(R("rl"), ind(R("loI"), LLt), R("mask"), OP.mult)
+        tt(R("rh"), ind(R("pk"), LLt), R("mask"), OP.mult)
+        mm(R("PSF", 0, 16), R("rh", 0, 128), R("rh0"), True, False)
+        mm(R("PSF", 0, 16), R("rh", 128, 256), R("rh1"), False, True)
         ts(R("hI"), R("hJ"), 15, OP.bitwise_and)
-        mm(R("PSL", 0, 16), R("rl", 0, 128), R("rh0", 0, 16), True, False)
-        mm(R("PSL", 0, 16), R("rl", 128, 256), R("rh1", 0, 16), False, True)
         SX = "SX%d" % (t + 1)
-        act(R(SX, 0, 256), ind(R("Zp"), R("zu")), FN.Copy)
-        tt(R("nB"), R("np1"), R("hI"), OP.subtract)
         tt(R(SX, 272, 288), R("np1"), R("hI"), OP.subtract)
-        cp(R(SX, 256, 272), R("PSL", 0, 16))
+        tt(R("zf"), R("zbase"), R("PSF", 0, 16), OP.subtract)
+        cp(R("pI"), R("PSF", 0, 16))
+        ts(R("zu"), R("zf"), 0.0625, OP.mult)
+        act(R(SX, 0, 256), ind(R("Zp"), R("zu")), FN.Copy)
+        ts(R("rA"), R("pI"), 15, OP.bitwise_and)
+        ts(R("M4"), R("pI"), 16.0, OP.is_lt, 4096.0, OP.mult)
+        ts(R("mA"), R("pI"), 4, OP.arith_shift_right)
+        tt(R(SX, 256, 272), R("rA"), R("M4"), OP.max)
+        cp(R("mB"), R("mA"))
         send(R(SX), R("X%d" % (t + 1)), "rx%d" % (t + 1))
-
-        last = t == TV - 1
-        step = 0 if last else SIG[t + 1] - SIG[t]
-        HI, LO = R("P%d" % step) if step else R("Ih"), R("N%d" % step)
-        full = 256 if last else 240
+        act(R("mrep"), ind(R("mB"), R("l16")), FN.Copy)
+        ts(R("sI"), R("vI"), 4095, OP.bitwise_and)
 
         def width(h):
             return min(full, 256 - 16 * h)
 
         def pen(h):
-            act(R("pen%d" % h, 0, width(h)), R("PSA", 0, width(h)), FN.Abs, float(h - 16 if h else 0))
+            act(R("pen%d" % h, 0, width(h)), R("mrep", 0, width(h)), FN.Abs, float(h - 16 if h else 0))
 
         def close_pe(k, h):
-            o, n = R(CB[k], 0, width(h)), width(h)
-            mm(o, HI, R("w16", 16 * h, 16 * h + n), True, False)
-            mm(o, LO, R("pen%d" % h, 0, n), False, True)
+            mm(R(CB[k], 0, width(h)), LO, R("pen%d" % h, 0, width(h)), False, True)
 
         def close_v(k, h):
             n = width(h)
@@ -529,8 +566,6 @@ def rank_program(g, core, T, topo):
             else:
                 tt(R("acc", 0, n), R(CB[k], 0, n), R("acc", 0, n), OP.max)
 
-        HS = (0, 1, 2, 4, 8)
-        CB = ("PS0", "PS1", "PSD", "PST", "PS0")
         for h in HS:
             pen(h)
         if not last:
@@ -539,31 +574,35 @@ def rank_program(g, core, T, topo):
                     close_pe(0, 0)
                     close_pe(1, 1)
                     close_pe(2, 2)
-                    close_pe(3, 4)
-                    close_v(0, 0)
                     run("v", lambda: g.vector.tensor_reduce(ap(R("cnt", 0, 1)), ap(R("M4")), AxisListType.X, OP.add), [R("cnt", 0, 1)], [R("M4")])
-                elif k == 1:
-                    close_pe(4, 8)
-                    mm(R("PSF", 0, 1), R("onf"), R("cnt", 0, 1), True, True)
-                elif k == 2:
-                    send(R("SZ%d" % (t + 1)), R("Z%d" % (t + 1)), "rz%d" % (t + 1))
+                    close_v(0, 0)
                     close_v(1, 1)
+                elif k == 1:
+                    close_pe(3, 4)
+                    close_pe(4, 8)
+                    mm(R("PSD", 0, 1), R("onf"), R("cnt", 0, 1), True, True)
                     close_v(2, 2)
                     close_v(3, 4)
+                elif k == 2:
                     close_v(4, 8)
-                    ts(R("SY%d" % (t + 1), 16, 256), R("acc", 0, 240), 2048.0, OP.add)
-                else:
+                    ts(R("SY%d" % (t + 1), 0, 240), R("acc", 0, 240), 2048.0, OP.add)
                     send(R("SY%d" % (t + 1)), R("Y%d" % (t + 1)), "ry%d" % (t + 1))
-                    ts(R("amI", 0, 1), R("PSF", 0, 1), -1.0 / 4096, OP.mult, 2048.0, OP.add)
+                    if t == 0:
+                        table(2)
+                        table(3)
+                else:
+                    send(R("SZ%d" % (t + 1)), R("Z%d" % (t + 1)), "rz%d" % (t + 1))
+                    ts(R("amI", 0, 1), R("PSD", 0, 1), -1.0 / 4096, OP.mult, 2048.0, OP.add)
                     ts(R("amJ", 0, 1), R("amI", 0, 1), 15, OP.bitwise_and)
                     cp(R("amc", 1, 2), R("amJ", 0, 1))
                     ts(R("B1"), R("thB", 16 * t + 16, 16 * t + 32), R("amc", 1, 2), OP.add)
-            post(t + 1, "SY%d" % (t + 1), "SZ%d" % (t + 1), fill)
+            post(t + 1, "SY%d" % (t + 1), "SZ%d" % (t + 1), R(SX, 272, 288), fill)
         else:
             for k, h in enumerate(HS):
                 close_pe(k, h)
                 close_v(k, h)
             cp(R("sfo"), R("sI"))
+            cp(R("nB"), R(SX, 272, 288))
             cp(R("a16"), R("acc"))
             for h in range(2):
                 mm(R("PSF", 128 * h, 128 * h + 128, p1=8), R("nB", 8 * h, 8 * h + 8), R("If"), True, True)
@@ -575,8 +614,16 @@ def rank_program(g, core, T, topo):
                         mm(o, R("S%d%d" % (g2, c2)), R("a16", 2 * b + c2, 256, 16), c2 == 0, c2 == 1)
             act(R("yns", p1=8), R("PSF", p1=8), FN.Copy)
             act(R("ywx"), R("PSR", 0, 256), FN.Copy, bias=2048.0)
-            change(TV)
-            dma("y", T.yx[:], T.xt[:, 0:4096], [], [R("xt", 0, 4096)])
+            last_x = "X%d" % TV
+            tt(R("colf"), R(last_x, 256, 272), R("base"), OP.add)
+            cp(R("colu"), R("colf"))
+            tt(R("sm"), ind(R("xt"), R("colu")), R(last_x, 0, 256), OP.add)
+            ts(R("colv"), R("colf", 8, 16), -2048.0, OP.add)
+            ts(R("nv"), R("sm"), 0.5, OP.mult, -0.25, OP.add)
+            cp(ind(R("xt", 0, 6144), R("colu", 0, 8)), R("nv", 0, 128))
+            cp(ind(R("xt", 2048, 8192), R("colv")), R("nv", 128, 256))
+            for q, c0 in (("y", 0), ("s", 2048)):
+                dma(q, T.yx[:, c0:c0 + 2048], T.xt[:, c0:c0 + 2048], [], [R("xt", c0, c0 + 2048)])
             vtr(R("yws"), R("ywx"))
             k = 8 - SIG[t]
             for y, c0 in ((T.yn, 0), (T.ys, 256)):

from concourse.bass import DstId
from concourse.mybir import AluOpType, AxisListType, ActivationFunctionType

OP = AluOpType
FN = ActivationFunctionType
SIG = [0, 1, 2, 3, 5, 6]
TV = 6
POS = {(8, 0): 0, (8, 1): 1, (4, 0): 2, (8, 2): 3, (8, 3): 4, (4, 1): 5, (2, 0): 6,
       (8, 4): 7, (8, 5): 8, (4, 2): 9, (8, 6): 10, (8, 7): 11, (4, 3): 12, (2, 1): 13, (1, 0): 14}
SHORT = [(2, 1), (4, 1), (4, 3), (4, 2), (1, 0), (2, 0), (4, 0)]
LONG = [1, 3, 5, 7, 2, 6, 0, 4]

SCRATCH = {}
TILE = {}
_ARENA = {"int32": "ari", "float32": "arf", "bfloat16": "arb", "float16": "arh", "uint16": "aru"}
_USED = {k: 0 for k in _ARENA}


def _b(name, cols, dtype, where="sbuf"):
    if where == "sbuf" and name[0] not in "XYZC" and name[:2] not in ("SX", "SY", "SZ", "SC") and name != "xt":
        TILE[name] = (_ARENA[dtype], _USED[dtype], cols)
        _USED[dtype] += (cols + 15) // 16 * 16
        SCRATCH[_ARENA[dtype]] = ("sbuf", [128, _USED[dtype]], dtype)
    else:
        TILE[name] = (name, 0, cols)
        SCRATCH[name] = (where, [128, cols], dtype)


for _n, _c in (("lsi", 2048), ("wdi", 256), ("sdi", 256), ("nli", 256), ("thi", 8), ("wti", 8), ("ioi", 256), ("pi", 16), ("gi", 256),
               ("g96", 96), ("lli", 96), ("llh", 96), ("vI", 16), ("hI", 16), ("hJ", 16), ("mI", 16), ("sI", 16), ("rI", 16), ("q16", 16), ("pk", 16), ("pI", 16), ("mA", 16), ("rA", 16), ("sq", 16), ("sq5", 16), ("w1", 16),
               ("kI", 16), ("cc", 16), ("cI", 16), ("nv", 256), ("amI", 8), ("amJ", 8), ("xii", 256)):
    _b(_n, _c, "int32")
for _n, _c in (("lsf", 2048), ("sdf", 256), ("nlf", 256), ("pc", 32), ("xi", 256), ("fi", 128), ("If", 128), ("onf", 128),
               ("thd", 96), ("thB", 96), ("base", 16), ("zbase", 16), ("d0s", 256), ("l15f", 16),
               ("colf", 16), ("dg", 256), ("lsc", 256), ("np1", 16), ("en", 64), ("thr", 64), ("B1", 16), ("Bt", 240), ("amc", 8),
               ("gif", 128), ("gd", 128), ("ge", 128), ("BOf", 128), ("Lmf", 256), ("u0", 16), ("u1", 16), ("u2", 16), ("u3", 16), ("u4", 16), ("u5", 16), ("u6", 16),
               ("zf", 16), ("M4", 16), ("cnt", 8), ("nB", 16), ("acc", 256), ("sfo", 16), ("ywx", 256), ("yws", 256), ("yns", 512)):
    _b(_n, _c, "float32")
for _n, _c in (("xt", 8192), ("I", 128), ("NI", 128), ("I5", 128), ("rB", 16), ("rd", 256), ("rh0", 16), ("rh1", 16), ("mB", 16), ("mrep", 256), ("mask", 256), ("zr", 2048), ("mc", 80), ("lc", 128), ("on", 96), ("onm", 96),
               ("wtb", 96), ("G8", 2048), ("Zp", 2064), ("d8", 2304), ("r8", 2048),
               ("pen0", 256), ("pen1", 256), ("pen2", 256), ("pen4", 256), ("pen8", 256), ("N0", 128), ("N1", 128), ("N2", 128), ("ab", 1792), ("sm", 256), ("good", 240), ("m1", 112), ("m2", 48), ("b8", 16), ("rh", 256), ("rl", 256), ("rq", 256)):
    _b(_n, _c, "bfloat16")
for _n, _c in (("Ih", 128), ("P1", 128), ("P2", 128), ("S00", 128), ("S01", 128), ("S10", 128), ("S11", 128),
               ("BO", 128), ("rg0", 16), ("rg1", 16), ("w16", 256), ("wd16", 256), ("x16", 256), ("Lm", 256), ("rcf", 256), ("a16", 256)):
    _b(_n, _c, "float16")
for _n, _c in (("ll", 96), ("l15", 16), ("l16", 16), ("colu", 16), ("colv", 8), ("off0", 16), ("zu", 16)):
    _b(_n, _c, "uint16")
for _t in range(1, TV + 1):
    _b("X%d" % _t, 288, "bfloat16")
    _b("SX%d" % _t, 288, "bfloat16")
for _t in range(TV):
    _b("Y%d" % _t, 256, "uint16")
    _b("Z%d" % _t, 288, "bfloat16")
    if _t:
        _b("SY%d" % _t, 256, "uint16")
        _b("SZ%d" % _t, 288, "bfloat16")
for _n in ("PS0", "PS1", "PSD", "PST", "PSA", "PSL", "PSR", "PSF"):
    _b(_n, 512, "float32", "psum")
PSUM = ("PS0", "PS1", "PSD", "PST", "PSA", "PSL", "PSR", "PSF")

SEMAPHORES = ["cv", "cs", "cp", "cg", "snt"] + ["d%d" % k for k in range(16)] + ["rx%d" % t for t in range(1, TV + 1)] + ["ry%d" % t for t in range(1, TV)] + ["rz%d" % t for t in range(1, TV)]


def R(name, c0=0, c1=None, step=1, p0=0, p1=128):
    buf, base, cols = TILE[name]
    return (buf, base + c0, base + (cols if c1 is None else c1), step, p0, p1)


def rank_program(g, core, T, topo):
    rank = T.rank_of(core)
    if rank is None:
        return
    n_ranks = len(T.cores)
    dst = T.cores[(rank + 1) % n_ranks]
    emask = topo.mask(core, dst)
    neng = len(topo.engines(core, dst))
    rid, pid, _se = topo.addr(dst)
    Q = {"v": g.vector, "s": g.scalar, "p": g.tensor, "g": g, "y": g.sync}
    SEMOF = {"v": "cv", "s": "cs", "p": "cp", "g": "cg"}
    count = {}
    known = {q: {} for q in Q}
    snap = {}
    log = {}
    nd = [0]

    def ap(r):
        name, c0, c1, step, p0, p1 = r
        if step == 1:
            return T[name][p0:p1, c0:c1]
        return T[name][p0:p1, c0:c1:step]

    def wait(q, sem, val):
        if known[q].get(sem, 0) >= val:
            return
        Q[q].wait_ge(T.sem[sem], val)
        known[q][sem] = val
        for s2, v2 in snap.get((sem, val), {}).items():
            if known[q].get(s2, 0) < v2:
                known[q][s2] = v2

    def meet(a, b):
        if a[4] >= b[5] or b[4] >= a[5] or a[1] >= b[2] or b[1] >= a[2]:
            return False
        return not (a[3] == b[3] and a[3] > 1 and (a[1] - b[1]) % a[3] != 0)

    def covers(a, b):
        return a[3] == 1 and a[4] <= b[4] and a[5] >= b[5] and a[1] <= b[1] and a[2] >= b[2]

    def order(q, reads, writes, eng):
        for r in reads:
            ps = r[0] in PSUM
            for (o, kind, sem, val, e) in log.get(r[0], []):
                if ps:
                    if (kind == "w" or e != eng) and not (e == eng == "p"):
                        wait(q, sem, val)
                elif kind == "w" and meet(r, o):
                    wait(q, sem, val)
        for r in writes:
            ps = r[0] in PSUM
            for (o, kind, sem, val, e) in log.get(r[0], []):
                if ps:
                    if e != eng:
                        wait(q, sem, val)
                elif meet(r, o) and (kind == "w" or e != eng):
                    wait(q, sem, val)

    def note(reads, writes, sem, val, eng):
        for r in writes:
            if r[0] in PSUM:
                if any(e != eng for (_o, _k, _s, _v, e) in log.get(r[0], [])):
                    log[r[0]] = []
            old = [x for x in log.get(r[0], []) if not covers(r, x[0])]
            log[r[0]] = old + [(r, "w", sem, val, eng)]
        for r in reads:
            old = [x for x in log.get(r[0], []) if not (x[1] == "r" and x[4] == eng and covers(r, x[0]))]
            log[r[0]] = old + [(r, "r", sem, val, eng)]

    def run(eng, fn, writes, reads):
        order(eng, reads, writes, eng)
        sem = SEMOF[eng]
        val = count.get(sem, 0) + 1
        count[sem] = val
        snap[(sem, val)] = dict(known[eng])
        fn().then_inc(T.sem[sem], 1)
        note(reads, writes, sem, val, eng)

    def dma(q, out, in_, writes, reads):
        order(q, reads, writes, "d")
        sem = "d%d" % nd[0]
        nd[0] += 1
        count[sem] = 16
        snap[(sem, 16)] = dict(known[q])
        Q[q].dma_start(out, in_).then_inc(T.sem[sem], 16)
        note(reads, writes, sem, 16, sem)

    def send(src, land, sem):
        order("g", [src], [], "r")
        count["snt"] = count.get("snt", 0) + neng
        g.remote_dma(ap(land), ap(src), T.sem[sem], T.sem.snt, pid, rid, emask)
        note([src], [], "snt", count["snt"], "r")
        count[sem] = neng
        note([], [land], sem, neng, sem)

    def opnd(x):
        if x[0] == "ind":
            return ap(x[1]).indirect(ap(x[2])), [x[1], x[2]]
        return ap(x), [x]

    def ind(win, off):
        return ("ind", win, off)

    def tt(out, a, b, op):
        (ia, ra), (ib, rb) = opnd(a), opnd(b)
        run("v", lambda: g.vector.tensor_tensor(ap(out), ia, ib, op), [out], ra + rb)

    def ts(out, a, s1, op0, s2=None, op1=None):
        ia, ra = opnd(a)
        rd = list(ra)
        v1, v2 = s1, s2
        if isinstance(s1, tuple):
            v1 = ap(s1)
            rd.append(s1)
        if isinstance(s2, tuple):
            v2 = ap(s2)
            rd.append(s2)
        if op1 is None:
            run("v", lambda: g.vector.tensor_scalar(ap(out), ia, v1, None, op0), [out], rd)
        else:
            run("v", lambda: g.vector.tensor_scalar(ap(out), ia, v1, v2, op0, op1), [out], rd)

    def cp(out, a):
        (ia, ra), (io, ro) = opnd(a), opnd(out)
        w = [out[1]] if out[0] == "ind" else [out]
        run("v", lambda: g.vector.tensor_copy(io, ia), w, ra + ro[1:])

    def ms(out, c):
        run("v", lambda: g.vector.memset(ap(out), c), [out], [])

    def scan(out, a, b, op0, op1):
        run("v", lambda: g.vector.tensor_tensor_scan(ap(out), ap(a), ap(b), 0.0, op0, op1), [out], [a, b])

    def vtr(out, a):
        run("v", lambda: g.vector.transpose(ap(out), ap(a)), [out], [a])

    def act(out, a, fn, bias=0.0, scale=1.0):
        ia, ra = opnd(a)
        sc = scale
        rd = list(ra)
        if isinstance(scale, tuple):
            sc = ap(scale)
            rd.append(scale)
        bi = bias
        if isinstance(bias, tuple):
            bi = ap(bias)
            rd.append(bias)
        run("s", lambda: g.scalar.activation(ap(out), ia, fn, bias=bi, scale=sc), [out], rd)

    def mm(out, lhsT, rhs, start, stop):
        run("p", lambda: g.tensor.matmul(ap(out), ap(lhsT), ap(rhs), start, stop), [out], [lhsT, rhs])

    def iota(out, pattern, base, cm):
        run("g", lambda: g.iota(ap(out), pattern, base, cm, allow_small_or_imprecise_dtypes=True), [out], [])

    for q, tile, src in (("y", R("sdi", p1=8), T.sd[:]), ("s", R("sdi", p0=8, p1=16), T.nl[:]), ("y", R("wdi"), T.wd[:]), ("s", R("xt", 0, 4096), T.x[:]),
                         ("s", R("lsi"), T.ls[:]), ("y", R("thi", 0, 1, p1=8), T.th[:]), ("y", R("wti", 0, 1), T.wt[:])):
        dma(q, ap(tile), src, [tile], [])

    iota(R("ioi"), [[1, 256]], 0, 0)
    iota(R("pi", 0, 1), [[1, 1]], 0, 1)
    iota(R("xi"), [[0, 16], [1, 16]], 0, 0)
    iota(R("lli", 0, 64), [[-1, 4], [0, 2], [1, 8]], 8, 0)
    iota(R("lli", 64, 96), [[-1, 2], [0, 2], [1, 8]], 8 - SIG[4], 0)
    iota(R("llh"), [[0, 6], [8, 2], [0, 8]], 0, 0)
    iota(R("g96", 0, 64), [[1, 4], [0, 2], [1, 8]], 0, 0)
    iota(R("g96", 64, 96), [[1, 2], [0, 2], [1, 8]], SIG[4], 0)
    iota(R("gif"), [[1, 8], [0, 16]], 0, 0)
    iota(R("onf"), [[0, 128]], 1, 0)
    iota(R("l15f", 0, 15), [[0, 15]], 0, 0)
    for (h, j), k in POS.items():
        if h < 8:
            iota(R("l15f", k, k + 1), [[0, 1]], {4: 16, 2: 32, 1: 48}[h], 0)
    for k, h in enumerate((1, 2, 4, 8)):
        iota(R("mc", 16 * k, 16 * k + 16), [[0, 16]], 16 - h, 2 * h - 16)
    iota(R("mc", 64, 80), [[0, 16]], 0, 0)
    iota(R("Zp", 2048, 2064), [[0, 16]], 0, 0)
    iota(R("xt", 6144, 8192), [[0, 2048]], 0, 0)
    for k in range(8):
        act(R("xt", 4096 + 256 * k, 4352 + 256 * k), R("xi"), FN.Copy, scale=0.0)
    iota(R("zr"), [[0, 256], [16, 8]], 0, 0)

    def pcol(k, p1=128):
        return R("pc", k, k + 1, p1=p1)

    def pint(k):
        return R("pi", k, k + 1)
    ts(pint(1), pint(0), 4, OP.arith_shift_right)
    ts(pint(2), pint(0), 15, OP.bitwise_and)
    ts(pint(3), pint(1), 1, OP.bitwise_and)
    cp(R("pc", 0, 3), R("pi", 0, 3))
    cp(R("fi"), R("ioi", 0, 128))
    ts(R("If"), R("fi"), pcol(0), OP.is_equal)
    cp(pcol(6), pint(3))
    ts(pcol(15), pcol(2), -1.0, OP.mult)
    ts(R("lli"), R("lli"), 7, OP.bitwise_and)
    tt(R("lli"), R("lli"), R("llh"), OP.add)
    cp(R("ll"), R("lli"))
    ts(R("mask"), R("xi"), pcol(2), OP.is_equal)
    ts(pcol(3), pcol(1), 8.0, OP.add)
    ts(R("rg0"), R("xi", 0, 16), pcol(1), OP.is_equal)
    ts(R("rg1"), R("xi", 0, 16), pcol(3), OP.is_equal)
    ts(pcol(16), pcol(1), -1.0, OP.mult)

    B16 = R

    def post(tn, Yd, Zd, n_at, fill):
        LLt = R("ll", 16 * tn, 16 * tn + 16)
        tt(B16("sq"), B16("sI"), B16("sI"), OP.mult)
        ts(B16("sq5"), B16("sq"), 5, OP.arith_shift_right)
        ts(B16("kI"), n_at, 77.0, OP.mult)
        cp(B16("rB"), B16("rI"))
        tt(B16("w1"), B16("sq5"), B16("sI"), OP.add)
        cp(R(Zd, 256, 272), B16("sI"))
        tt(B16("cc"), B16("w1"), B16("kI"), OP.add)
        ts(B16("cI"), B16("cc"), 2047, OP.bitwise_and)
        tt(R(Zd, 272, 288), B16("sI"), R(Zd, 256, 272), OP.subtract)
        tt(R("rcf"), ind(R("cI"), LLt), R("mask"), OP.mult)
        fill(0)
        mm(R("PSF", 0, 16), R("rcf", 0, 128), R("rg0"), True, False)
        mm(R("PSF", 0, 16), R("rcf", 128, 256), R("rg1"), False, True)
        fill(1)
        cp(R(Yd, 240, 256), R("PSF", 0, 16))
        fill(2)
        act(R("rq"), ind(R("rB"), LLt), FN.Copy)
        mm(R("PST", 0, 128), R("rq", 0, 128), R("I"), True, True)
        mm(R("PST", 128, 256), R("rq", 128, 256), R("I"), True, True)
        act(R("rd"), R("PST", 0, 256), FN.Abs, bias=pcol(15))
        act(R(Zd, 0, 256), R("rd"), FN.Relu, bias=1.0, scale=-1.0)
        fill(3)

    cp(R("sdf", p1=16), R("sdi", p1=16))
    for h in range(2):
        for k in range(2):
            mm(R("PSA", 16 * k + 8 * h, 16 * k + 8 * h + 8), R("sdf", 128 * h, 128 * h + 128, p1=16), R("If", 8 * k, 8 * k + 8, p1=16), True, True)
    act(R("I"), R("If"), FN.Copy)
    act(R("d0s"), R("xi"), FN.Sign)
    act(R("gd"), R("gif"), FN.Abs, bias=pcol(16))
    act(R("BOf"), R("gd"), FN.Relu, bias=1.0, scale=-1.0)
    ts(pcol(7), pcol(6), -1.0, OP.mult, 1.0, OP.add)
    ts(pcol(8), pcol(6), -32.0, OP.mult, 16.0, OP.add)
    tt(pcol(8), pcol(8), pcol(0), OP.add)
    ts(R("S00"), R("fi"), pcol(0), OP.is_equal, pcol(7), OP.mult)
    ts(R("S11"), R("fi"), pcol(0), OP.is_equal, pcol(6), OP.mult)
    ts(R("S01"), R("fi"), pcol(8), OP.is_equal, pcol(7), OP.mult)
    ts(R("S10"), R("fi"), pcol(8), OP.is_equal, pcol(6), OP.mult)
    cp(B16("sI"), R("PSA", 0, 16))
    cp(B16("nB"), R("PSA", 16, 32))
    ts(B16("rI"), B16("sI"), 15, OP.bitwise_and)
    post(0, "Y0", "Z0", R("nB"), lambda k: None)
    ts(R("wd16"), R("wdi"), -2048.0, OP.add)
    vtr(R("x16"), R("wd16"))
    for c in range(16):
        b, c2 = c // 2, c % 2
        o = R("PS0", c, 256, 16)
        for g2 in range(2):
            mm(o, R("S%d%d" % (c2, g2)), R("x16", 32 * b + 16 * g2, 32 * b + 16 * g2 + 16), g2 == 0, g2 == 1)
    ts(R("g96"), R("g96"), 7, OP.bitwise_and)
    ts(R("on"), R("g96"), pcol(1), OP.is_equal)
    cp(pcol(11), R("wti", 0, 1))
    act(R("NI"), R("I"), FN.Copy, scale=-1.0)
    act(R("onm"), R("on"), FN.Copy, scale=-1.0)
    act(R("I5"), R("I"), FN.Copy, scale=5.0)
    act(R("wtb"), R("on"), FN.Copy, scale=pcol(11))

    def later():
        ts(R("l15", 0, 15), R("l15f", 0, 15), pcol(2), OP.add)
        ts(R("l16"), R("xi", 0, 16), 0.0, OP.mult, pcol(2), OP.add)
        ts(pcol(10), pcol(2), 16.0, OP.mult)
        ts(R("base"), R("ioi", 0, 16), 256.0, OP.mult, pcol(10), OP.add)
        ts(R("zbase"), R("base"), 8.0, OP.mult, 247.5, OP.add)
        cp(pcol(13, 8), R("thi", 0, 1, p1=8))
        ts(R("thd", p1=8), R("g96", p1=8), pcol(0, 8), OP.is_equal, pcol(13, 8), OP.mult)
        mm(R("PSA", 0, 96), R("onf", p1=8), R("thd", p1=8), True, True)
        ts(pcol(14), pcol(0), 0.0, OP.is_equal, 131072.0, OP.mult)
        ts(pcol(9), pcol(0), 1.0, OP.is_equal)
        tt(pcol(9), pcol(9), pcol(14), OP.add)
        ts(R("lc"), R("onf"), pcol(9), OP.mult)
        ts(pint(4), pint(0), 16.0, OP.add)
        ts(pint(5), pint(0), 32.0, OP.add)
        ts(R("pi", 4, 6), R("pi", 4, 6), 127, OP.bitwise_and)
        cp(R("pc", 4, 6), R("pi", 4, 6))
        ts(R("rh0"), R("xi", 0, 16), pcol(1), OP.is_equal)
        ts(R("rh1"), R("xi", 0, 16), pcol(3), OP.is_equal)
        for name, k in (("P1", 4), ("P2", 5), ("Ih", 0)):
            ts(R(name), R("fi"), pcol(k), OP.is_equal)
        ts(R("BO"), R("gif"), pcol(1), OP.is_equal)
        ts(R("thB"), R("PSA", 0, 96), 1.0, OP.add)
        ts(R("pc", 17, 19), R("pc", 4, 6), -1.0, OP.mult)

    def negated():
        for name, k in (("N1", 17), ("N2", 18)):
            act(R("gd"), R("fi"), FN.Abs, bias=pcol(k))
            act(R("ge"), R("gd"), FN.Relu, bias=1.0, scale=-1.0)
            act(R(name), R("ge"), FN.Copy, scale=-4096.0)
        act(R("N0"), R("If"), FN.Copy, scale=-4096.0)

    def table(k):
        ts(R("lsf", 512 * k, 512 * k + 512), R("lsi", 512 * k, 512 * k + 512), -2048.0, OP.add)

    later()
    ts(R("Y0", 0, 240), R("PS0", 0, 240), 2048.0, OP.add)
    ts(R("thB"), R("PSA", 0, 96), 1.0, OP.add)

    def change(t):
        X = "X%d" % t
        tt(R("colf"), R(X, 256, 272), R("base"), OP.add)
        cp(R("colu"), R("colf"))
        tt(R("sm"), ind(R("xt"), R("colu")), R(X, 0, 256), OP.add)
        ts(R("nv"), R("sm"), 0.5, OP.mult, -0.25, OP.add)
        cp(ind(R("xt"), R("colu")), R("nv"))

    for t in range(TV):
        Y, Z = "Y%d" % t, "Z%d" % t
        ont = R("on", 16 * t, 16 * t + 8)
        wtt = R("wtb", 16 * t, 16 * t + 8)
        LLt = R("ll", 16 * t, 16 * t + 16)

        def row(j):
            return R("G8", j, 2048, 8)

        def off(j):
            return R("off0") if j == 0 else R(Y, 16 * j - 16, 16 * j)

        def gather(j):
            act(row(j), ind(R("xt"), off(j)), FN.Copy)

        def diff(k0, k1):
            for k in range(k0, k1):
                h, j = SHORT[k]
                o = R("PS%d" % (k // 2 % 2), 256 * (k % 2), 256 * (k % 2) + 256)
                mm(o, R("I"), row(j), True, False)
                mm(o, R("NI"), row(j + h), False, True)

        def absol(k0, k1):
            act(R("ab", 256 * k0, 256 * k1), R("PS%d" % (k0 // 2 % 2), 0, 256 * (k1 - k0)), FN.Abs)

        def dshort(k):
            c = 16 * POS[SHORT[k]]
            for h in range(2):
                mm(R("PSD", c + 8 * h, c + 8 * h + 8), R("ab", 256 * k + 128 * h, 256 * k + 128 * h + 128), ont, True, True)

        def long_(k):
            j = LONG[k]
            tt(R("d8", 256 * k, 256 * k + 256), ind(R("xt"), off(j + 8)), row(j), OP.subtract)

        def absl(k0, k1):
            act(R("r8", 256 * k0, 256 * k1), R("d8", 256 * k0, 256 * k1), FN.Abs)

        def dlong(k):
            c = 16 * POS[(8, LONG[k])]
            for h in range(2):
                a = 256 * k + 128 * h
                o = R("PSD", c + 8 * h, c + 8 * h + 8)
                if k >= 4:
                    mm(o, R("d8", a, a + 128), R("onm", 16 * t, 16 * t + 8), True, False)
                mm(o, R("r8", a, a + 128), ont, k < 4, True)

        def limits():
            n_in = R("X%d" % t, 272, 288) if t else R("nB")
            for k, h in enumerate((8, 4, 2, 1)):
                act(R("en", 16 * k, 16 * k + 16), n_in, FN.Sign, bias=1.5 - 2 * h)
            ts(R("np1"), n_in, 1.0, OP.add, 16.0, OP.min)
            for k in range(4):
                tt(R("thr", 16 * k, 16 * k + 16), R("en", 16 * k, 16 * k + 16), R("B1") if t else R("thB", 0, 16), OP.mult)

        if t:
            change(t)
        limits()
        for j in (1, 3, 5, 7):
            gather(j)
        gather(2)
        ts(R("w16", 16, 256), R(Y, 0, 240), -2048.0, OP.add)
        long_(0)
        diff(0, 1)
        if t:
            tt(R("Lm"), ind(R("lsf"), R(Y, 240, 256)), R(Z, 0, 256), OP.mult)
            mm(R("PSF", 0, 256), R("BO"), R("Lm"), True, True)
        else:
            tt(R("Lmf"), ind(R("lsi"), R(Y, 240, 256)), R(Z, 0, 256), OP.mult)
            mm(R("PSF", 0, 256), R("BOf"), R("Lmf"), True, True)
        diff(1, 2)
        diff(2, 3)
        mm(R("PST", 0, 80), R("lc"), R("mc"), True, False)
        mm(R("PST", 64, 80), R("I5"), R(Z, 256, 272), False, False)
        mm(R("PST", 64, 80), R("I5"), R(Z, 272, 288), False, False)
        long_(1)
        tt(R("dg"), R("PSF", 0, 256), R("mask"), OP.mult)
        scan(R("lsc"), R("d0s"), R("dg"), OP.mult, OP.add)
        ts(R("off0"), R("lsc", 15, 256, 16), 2048.0 if t else 0.0, OP.add)
        ts(R("w16", 0, 16), R("lsc", 15, 256, 16), 0.0 if t else -2048.0, OP.add)
        absol(0, 2)
        gather(6)
        gather(0)
        gather(4)
        long_(2)
        long_(3)
        long_(4)
        long_(5)
        diff(3, 4)
        dshort(0)
        dshort(1)
        absol(2, 4)
        absl(0, 2)
        diff(4, 6)
        dlong(0)
        dlong(1)
        dshort(2)
        dshort(3)
        absol(4, 6)
        absl(2, 4)
        scan(R("Zp", 0, 2048), R("zr"), R("G8"), OP.min, OP.max)
        tt(R("d8", 2048, 2304), ind(R("xt"), off(4)), row(0), OP.subtract)
        act(R("ab", 1536, 1792), R("d8", 2048, 2304), FN.Abs)
        ts(R("r8", 1024, 1536), R("d8", 1024, 1536), 0.0, OP.max, 2.0, OP.mult)
        long_(6)
        long_(7)
        ts(R("r8", 1536, 2048), R("d8", 1536, 2048), 0.0, OP.max, 2.0, OP.mult)
        act(R("Bt"), ind(R("thr"), R("l15", 0, 15)), FN.Copy)

        def terms(blocks):
            for a, k in blocks:
                for h in range(2):
                    mm(R("PST", 16 * a + 8 * h, 16 * a + 8 * h + 8), R("Zp", 1024 * h + k - 1, 1024 * h + 1024, 8), wtt, False, a == 3 and h == 1)
        dshort(4)
        dshort(5)
        terms(((0, 1), (4, 1), (1, 2)))
        dlong(2)
        dlong(3)
        dlong(4)
        dlong(5)
        dshort(6)
        dlong(6)
        dlong(7)
        terms(((2, 4), (3, 8)))
        last = t == TV - 1
        step = 0 if last else SIG[t + 1] - SIG[t]
        HI, LO = R("P%d" % step) if step else R("Ih"), R("N%d" % step)
        full = 256 if last else 240
        HS = (0, 1, 2, 4, 8)
        CB = ("PS0", "PS1", "PSA", "PSL", "PSR")
        for k, h in enumerate(HS):
            n = min(full, 256 - 16 * h)
            mm(R(CB[k], 0, n), HI, R("w16", 16 * h, 16 * h + n), True, False)
        if t == 0:
            negated()
            table(0)
            table(1)
        tt(R("good"), R("PSD", 0, 240), R("Bt"), OP.is_lt)
        tt(R("m1"), R("good", 0, 112), R("good", 112, 224), OP.mult)
        tt(R("u1"), R("PST", 0, 16), R("good", 224, 240), OP.mult)
        tt(R("m2"), R("m1", 0, 48), R("m1", 48, 96), OP.mult)
        tt(R("u2"), R("PST", 16, 32), R("m1", 96, 112), OP.mult)
        tt(R("b8"), R("m2", 0, 16), R("m2", 16, 32), OP.mult)
        tt(R("u3"), R("PST", 32, 48), R("m2", 32, 48), OP.mult)
        tt(R("u4"), R("PST", 64, 80), R("u1"), OP.max)
        tt(R("u5"), R("PST", 48, 64), R("b8"), OP.mult)
        tt(R("u0"), R("u2"), R("u3"), OP.max)
        tt(R("u6"), R("u4"), R("u5"), OP.max)
        tt(R("vI"), R("u0"), R("u6"), OP.max)
        ts(R("q16"), R("vI"), 13, OP.arith_shift_right, 240, OP.bitwise_and)
        ts(R("rI"), R("vI"), 15, OP.bitwise_and)
        ts(R("mI"), R("vI"), 17, OP.arith_shift_right)
        tt(R("pk"), R("q16"), R("rI"), OP.add)
        ts(R("hJ"), R("mI"), -1.0, OP.mult, 16.0, OP.add)
        tt(R("rh"), ind(R("pk"), LLt), R("mask"), OP.mult)
        mm(R("PSF", 0, 16), R("rh", 0, 128), R("rh0"), True, False)
        mm(R("PSF", 0, 16), R("rh", 128, 256), R("rh1"), False, True)
        ts(R("hI"), R("hJ"), 15, OP.bitwise_and)
        SX = "SX%d" % (t + 1)
        tt(R(SX, 272, 288), R("np1"), R("hI"), OP.subtract)
        tt(R("zf"), R("zbase"), R("PSF", 0, 16), OP.subtract)
        cp(R("pI"), R("PSF", 0, 16))
        ts(R("zu"), R("zf"), 0.0625, OP.mult)
        act(R(SX, 0, 256), ind(R("Zp"), R("zu")), FN.Copy)
        ts(R("rA"), R("pI"), 15, OP.bitwise_and)
        ts(R("M4"), R("pI"), 16.0, OP.is_lt, 4096.0, OP.mult)
        ts(R("mA"), R("pI"), 4, OP.arith_shift_right)
        tt(R(SX, 256, 272), R("rA"), R("M4"), OP.max)
        cp(R("mB"), R("mA"))
        send(R(SX), R("X%d" % (t + 1)), "rx%d" % (t + 1))
        act(R("mrep"), ind(R("mB"), R("l16")), FN.Copy)
        ts(R("sI"), R("vI"), 4095, OP.bitwise_and)

        def width(h):
            return min(full, 256 - 16 * h)

        def pen(h):
            act(R("pen%d" % h, 0, width(h)), R("mrep", 0, width(h)), FN.Abs, float(h - 16 if h else 0))

        def close_pe(k, h):
            mm(R(CB[k], 0, width(h)), LO, R("pen%d" % h, 0, width(h)), False, True)

        def close_v(k, h):
            n = width(h)
            if k == 0:
                ts(R("acc", 0, n), R("PS0", 0, n), -2048.0, OP.max)
            else:
                tt(R("acc", 0, n), R(CB[k], 0, n), R("acc", 0, n), OP.max)

        for h in HS:
            pen(h)
        if not last:
            def fill(k):
                if k == 0:
                    close_pe(0, 0)
                    close_pe(1, 1)
                    close_pe(2, 2)
                    run("v", lambda: g.vector.tensor_reduce(ap(R("cnt", 0, 1)), ap(R("M4")), AxisListType.X, OP.add), [R("cnt", 0, 1)], [R("M4")])
                    close_v(0, 0)
                    close_v(1, 1)
                elif k == 1:
                    close_pe(3, 4)
                    close_pe(4, 8)
                    mm(R("PSD", 0, 1), R("onf"), R("cnt", 0, 1), True, True)
                    close_v(2, 2)
                    close_v(3, 4)
                elif k == 2:
                    close_v(4, 8)
                    ts(R("SY%d" % (t + 1), 0, 240), R("acc", 0, 240), 2048.0, OP.add)
                    send(R("SY%d" % (t + 1)), R("Y%d" % (t + 1)), "ry%d" % (t + 1))
                    if t == 0:
                        table(2)
                        table(3)
                else:
                    send(R("SZ%d" % (t + 1)), R("Z%d" % (t + 1)), "rz%d" % (t + 1))
                    ts(R("amI", 0, 1), R("PSD", 0, 1), -1.0 / 4096, OP.mult, 2048.0, OP.add)
                    ts(R("amJ", 0, 1), R("amI", 0, 1), 15, OP.bitwise_and)
                    cp(R("amc", 1, 2), R("amJ", 0, 1))
                    ts(R("B1"), R("thB", 16 * t + 16, 16 * t + 32), R("amc", 1, 2), OP.add)
            post(t + 1, "SY%d" % (t + 1), "SZ%d" % (t + 1), R(SX, 272, 288), fill)
        else:
            for k, h in enumerate(HS):
                close_pe(k, h)
                close_v(k, h)
            cp(R("sfo"), R("sI"))
            cp(R("nB"), R(SX, 272, 288))
            cp(R("a16"), R("acc"))
            for h in range(2):
                mm(R("PSF", 128 * h, 128 * h + 128, p1=8), R("nB", 8 * h, 8 * h + 8), R("If"), True, True)
                mm(R("PSF", 256 + 128 * h, 384 + 128 * h, p1=8), R("sfo", 8 * h, 8 * h + 8), R("If"), True, True)
            for b in range(8):
                for g2 in range(2):
                    o = R("PSR", 32 * b + 16 * g2, 32 * b + 16 * g2 + 16)
                    for c2 in range(2):
                        mm(o, R("S%d%d" % (g2, c2)), R("a16", 2 * b + c2, 256, 16), c2 == 0, c2 == 1)
            act(R("yns", p1=8), R("PSF", p1=8), FN.Copy)
            act(R("ywx"), R("PSR", 0, 256), FN.Copy, bias=2048.0)
            last_x = "X%d" % TV
            tt(R("colf"), R(last_x, 256, 272), R("base"), OP.add)
            cp(R("colu"), R("colf"))
            tt(R("sm"), ind(R("xt"), R("colu")), R(last_x, 0, 256), OP.add)
            ts(R("colv"), R("colf", 8, 16), -2048.0, OP.add)
            ts(R("nv"), R("sm"), 0.5, OP.mult, -0.25, OP.add)
            cp(ind(R("xt", 0, 6144), R("colu", 0, 8)), R("nv", 0, 128))
            cp(ind(R("xt", 2048, 8192), R("colv")), R("nv", 128, 256))
            for q, c0 in (("y", 0), ("s", 2048)):
                dma(q, T.yx[:, c0:c0 + 2048], T.xt[:, c0:c0 + 2048], [], [R("xt", c0, c0 + 2048)])
            vtr(R("yws"), R("ywx"))
            k = 8 - SIG[t]
            for y, c0 in ((T.yn, 0), (T.ys, 256)):
                for b0, b1, g0, g1 in ((SIG[t], 8, 0, k), (0, SIG[t], k, 8)):
                    r = R("yns", c0, c0 + 256, p0=g0, p1=g1)
                    dma("s", y[b0:b1, :], ap(r), [], [r])
            dma("y", T.yw[:], ap(R("yws")), [], [R("yws")])
    for sem in SEMAPHORES:
        if count.get(sem, 0):
            wait("g", sem, count[sem])
